import numpy as np, ml_dtypes
CORES = [13,21,141,149]
N = 4
BF = ml_dtypes.bfloat16
W, L, RO, PX, LIM = 3072, 192, 4, 3, 12
def parts(rng):
    X = rng.integers(0, 64, (N, 8, 16, W)); H = rng.integers(0, 2 * W, (N, 8, 16, L)); c = rng.integers(0, W, (N, 8, L)); z = rng.integers(0, 64, (N, 8, 16, L))
    return X, H, c, z, np.argsort(rng.random((N, 8, W)), axis=-1).astype(np.int64)
def pack(X, H, c, z, nx):
    return {"xt": np.ascontiguousarray(X.reshape(N, 128, W)).astype(np.float32).astype(BF), "mem": np.ascontiguousarray(H.reshape(N, 128, L)).astype(np.int32),
            "plc": np.ascontiguousarray(c).astype(np.int32), "zt": np.ascontiguousarray(z.reshape(N, 128, L)).astype(np.float32).astype(BF), "nxt": np.ascontiguousarray(nx).astype(np.int32)}
def choose(X, H, c, z, pen):
    e = H >> 1; d = np.where((H & 1) == 1, -e, e); cc = c[:, :, None, :]
    pl = np.concatenate([(cc + d) % W, (cc - d) % W], axis=2); co = []
    for h in (0, 1):
        v = np.take_along_axis(X, np.ascontiguousarray(pl[:, :, 16 * h:16 * h + 16]).reshape(N, 8, 1, 16 * L), 3).reshape(N, 8, 16, 16, L)
        co.append(np.add.reduce(np.abs(v - z[:, :, :, None, :]), axis=2) + 4 * np.arange(16)[:, None] + h * pen[:, None, None, None])
    return pl, np.argmin(np.concatenate(co, axis=2), axis=2)
def setup_inputs(rng):
    return pack(*parts(rng))
def setup_inputs_corners(rng):
    X, H, c, z, nx = parts(rng); far = np.array([0, 1, W // 2 - 1, W // 2, W // 2 + 1, W - 1]); spots = np.array([0, 1, W // 2, W - 1])
    for p in range(N):
        for g in range(8):
            k = (p + g) % 8
            if k == 0: H[p, g] = 2 * rng.choice(far, (16, L)) + rng.integers(0, 2, (16, L)); c[p, g] = rng.choice(spots, L)
            if k == 1: H[p, g] = H[p, g, :1].copy()
            if k == 2: H[p, g] = 2 * (H[p, g, :1] >> 1) + (np.arange(16) % 2)[:, None]
            if k == 3: nx[p, g] = np.arange(W); c[p, g] = rng.choice(spots, L)
            if k == 4: nx[p, g] = rng.choice(np.array([0, W - 1]), W)
            if k == 5: nx[p, g] = (np.arange(W) + 1) % W; H[p, g] = rng.integers(0, 4, (16, L))
            if k == 6: H[p, g] = np.where(rng.random((1, L)) < 0.5, 0, 2 * W - 1)
            if k == 7: c[p, g] = rng.choice(spots, L); X[p, g] = rng.integers(0, 64, (16, 3))[:, rng.integers(0, 3, W)]
    return pack(X, H, c, z, nx)
def setup_inputs_crowd(rng):
    X, H, c, z, nx = parts(rng); few = int(rng.integers(1, 4))
    for p in range(N):
        for g in range(8):
            P = rng.permutation(np.arange(1, W - 1))[:3]; k = (p + g) % 5
            if g % 4 == 0: P[0] = 0
            if g % 4 == 3: P[0] = W - 1
            near = p >= N - 2 and g == (-p) % 5
            if near:
                x0 = np.full(16, 32) if p == N - 2 else X[p, g][:, P[0]].copy()
                far = np.full(16, 62) if p == N - 2 else np.minimum((x0 + 32) % 64, 62)
                X[p, g] = far[:, None] + rng.integers(0, 2, (16, W)) * (np.arange(16) < 4)[:, None]; X[p, g, :, P[0]] = x0
            to = np.full(L, P[0])
            if k == 1: to[0] = P[1]
            if k == 2: to[L - 1] = P[1]
            if k == 3: to = P[rng.integers(0, 3, L)]
            if k == 4: to = rng.permutation(W)[:L]
            if p == N - 2:
                H[p, g] = rng.integers(0, 2, (16, L)); c[p, g] = to; z[p, g] = np.where(X[p, g][:, to] < 32, 63, 0)
                if near:
                    for i in (L - 1, 0, L // 2)[:few]:
                        e = int(rng.integers(1, W // 2)); s = int(rng.integers(0, 2))
                        H[p, g, 0, i] = 2 * e + s; c[p, g, i] = (P[0] + (-e if s == 1 else e)) % W
                continue
            rev = np.full(L, 1) if p in (0, N - 1) else (rng.permutation(L) < L // 2 - int(g == 7)).astype(np.int64)
            if p == N - 1 and g == 7: rev[L - 1] = 0
            e = rng.integers(1, W // 2, L); s = rng.integers(0, 2, L); d = np.where(s == 1, -e, e)
            c[p, g] = (to + np.where(rev == 1, d, -d)) % W; H[p, g, 0] = 2 * e + s
            z[p, g] = np.clip(X[p, g][:, to] + rng.integers(-2, 3, (16, L)), 0, 63)
    return pack(X, H, c, z, nx)
def setup_inputs_ends(rng):
    X = np.where(rng.random((N, 8, 1, W)) < 0.5, 63 * rng.integers(0, 2, (N, 8, 1, W)), 63 * rng.integers(0, 2, (N, 8, 16, W)))
    z = np.where(rng.random((N, 8, 1, L)) < 0.5, 63 * rng.integers(0, 2, (N, 8, 1, L)), 63 * rng.integers(0, 2, (N, 8, 16, L)))
    H = (2 * W - 1) * rng.integers(0, 2, (N, 8, 16, L)); c = (W - 1) * rng.integers(0, 2, (N, 8, L)); nx = (W - 1) * rng.integers(0, 2, (N, 8, W))
    o = rng.integers(0, 2, (N, 8)); o[:, 7] = 1; nx[:, :, 0] = (W - 1) * o; nx[:, :, W - 1] = (W - 1) * (1 - o)
    for q in (0, 1, W - 2, W - 1):
        X[:, 1, :, q] = 63; X[:, 6, :, q] = 0; X[:, 7, :, q] = 0 if q < 2 else 63
    z[:, 1] = 63 * rng.integers(0, 2, (N, 1, L)); z[:, 6] = 63 * rng.integers(0, 2, (N, 1, L))
    for i in (0, 1, L - 1): z[:, 1, :, i] = 0; z[:, 6, :, i] = 63
    rest = np.add.reduce((choose(X, H, c, z, np.zeros(N, np.int64))[1] >> 4)[:, :7].reshape(N, -1), axis=1)
    for p in range(N):
        n = 32 + ((0 if p == 1 else 31) - int(rest[p])) % 32
        m = np.zeros(L, bool); m[0] = True; m[L - 1] = True; m[rng.permutation(np.arange(1, L - 1))[:n - 2]] = True
        cc = (W - 1) * rng.integers(0, 2, L); cc[m] = 0; zz = 63 * rng.integers(0, 2, L); zz[m] = 63; zz[(~m) & (cc == 0)] = 0
        c[p, 7] = cc; z[p, 7] = zz[None, :]; H[p, 7, 0] = np.where(m | (zz == 0), 2 * W - 1, 0)
        for i in (0, L - 1): H[p, 7, 12:, i] = 2 * W - 1
    return pack(X, H, c, z, nx)
def setup_inputs_spread(rng):
    X = np.minimum((np.exp2(6 * rng.random((N, 8, 1, W))) * rng.random((N, 8, 16, W))).astype(np.int64), 63)
    z = np.minimum((np.exp2(6 * rng.random((N, 8, 1, L))) * rng.random((N, 8, 16, L))).astype(np.int64), 63)
    e = np.clip(np.power(float(W), rng.random((N, 8, 16, L))).astype(np.int64) - 1, 0, W - 1)
    H = 2 * e + (rng.random((N, 8, 16, L)) < rng.random((N, 8, 1, 1))).astype(np.int64)
    c = np.minimum((W * rng.random((N, 8, L)) ** 3).astype(np.int64), W - 1); nx = np.minimum((W * rng.random((N, 8, W)) ** 2).astype(np.int64), W - 1)
    return pack(X, H, c, z, nx)
def setup_inputs_ties(rng):
    X, H, c, z, nx = parts(rng)
    X[:, 2:7] = 4 * rng.integers(0, 12, (N, 1, 16, 1)) + 4 * rng.integers(0, 3, (N, 5, 16, W)) * (np.arange(16) < 2)[:, None]
    z[:, 2:7] = 4 * rng.integers(0, 16, (N, 5, 16, L)); X[:, 7] = rng.integers(0, 64, (N, 16, 1)); X[:, :2] = 0
    X[:, 6] = 63 - (np.argsort(rng.random((N, 16, W)), axis=1) < rng.integers(0, 9, (N, 1, W))).astype(np.int64); z[:, 6] = 0
    o = N - 1 if PX < N - 1 else PX - 1
    X[o, 6] = 63 - X[o, 6]
    for p in range(N):
        if p < (p ^ PX):
            lo = rng.integers(0, 63 - LIM, (2, 16, L)); n = rng.choice(np.array([0, 7, 8, 9, 10, 16]), (2, 1, L))
            hi = lo + np.where(np.argsort(rng.random((2, 16, L)), axis=1) < n, LIM, LIM + 1); sw = rng.random((2, 1, L)) < 0.5
            z[p, :2] = np.where(sw, hi, lo); z[p ^ PX, :2] = np.where(sw, lo, hi)
    return pack(X, H, c, z, nx)
def check_inputs(d):
    bad = []
    for k, hi in (("xt", 63), ("mem", 2 * W - 1), ("plc", W - 1), ("zt", 63), ("nxt", W - 1)):
        v = np.asarray(d[k]).astype(np.float64)
        if not (np.min(v) >= 0 and np.max(v) <= hi): bad.append("range of " + k)
        elif np.any(v != np.floor(v)): bad.append("whole numbers in " + k)
    return bad
def reference(xt, mem, plc, zt, nxt):
    X = xt.astype(np.float32).astype(np.int64).reshape(N, 8, 16, W); nx = nxt.astype(np.int64)
    H = mem.astype(np.int64).reshape(N, 8, 16, L); c = plc.astype(np.int64); z = zt.astype(np.float32).astype(np.int64).reshape(N, 8, 16, L)
    A = np.zeros(N, np.int64); par = np.arange(N) ^ PX
    for t in range(RO):
        if t > 0: H = np.roll(H, 1, axis=0); c = np.roll(c, 1, axis=0); z = np.roll(z, 1, axis=0)
        pl, w = choose(X, H, c, z, A & 31); rev = w >> 4
        q = np.take_along_axis(pl, w[:, :, None, :], 2)[:, :, 0]
        step = np.take_along_axis(H, (w & 15)[:, :, None, :], 2) ^ rev[:, :, None, :]
        A = np.add.reduce(rev.reshape(N, -1), axis=1)
        xq = np.take_along_axis(X, q[:, :, None, :], 3); half = (xq + z) >> 1
        u, first = np.unique((np.arange(N * 8).reshape(N, 8, 1) * W + q).reshape(-1), return_index=True)
        X[u // (8 * W), (u // W) % 8, :, u % W] = half.transpose(0, 1, 3, 2).reshape(-1, 16)[first]
        z = np.abs(z - xq); c = np.take_along_axis(nx, q, 2)
        H = np.concatenate([step, H[:, :, :15]], axis=2)
        alike = np.add.reduce((np.abs(z - z[par]) <= LIM).astype(np.int64), axis=2) >= 9
        H = np.concatenate([H[:, :, :8], np.where(alike[:, :, None, :], H[par][:, :, 8:], H[:, :, 8:])], axis=2)
    return {"yx": X.reshape(N, 128, W).astype(np.float32).astype(BF), "yh": H.reshape(N, 128, L).astype(np.float32), "yc": c.astype(np.float32), "yz": z.reshape(N, 128, L).astype(np.float32).astype(BF)}

@@ -1,0 +1,591 @@
+from concourse.mybir import AluOpType, AxisListType, ActivationFunctionType
+
+ALU = AluOpType
+ACT = ActivationFunctionType
+W, L, NV = 3072, 192, 4
+F32, BF, I32, U16 = "float32", "bfloat16", "int32", "uint16"
+C0, C2, U0, UH, UF, UN, UP, RBW = 0, 12, 24, 120, 216, 312, 328, 424
+T1, T2, TE = 16, 16 + W, 32 + 2 * W
+
+
+def sb(w, dt=F32):
+    return ("sbuf", [128, w], dt)
+
+
+SCRATCH = {
+    "TB": sb(TE, BF), "NX": sb(W, I32), "IW": sb(W), "XB": sb(32 * L, BF), "EB": sb(32 * L, BF),
+    "HC": sb(384, I32), "UC": sb(384), "TI": sb(768), "TO": sb(768),
+    "WI": sb(304, I32), "WJ": sb(304, I32), "WF": sb(304), "WG": sb(304), "MM": sb(304), "FO": sb(384),
+    "FM": sb(L), "FN": sb(L), "FH": sb(L), "CB": sb(L),
+    "OF": sb(384), "OT": sb(384), "OM": sb(384), "OU": sb(384, U16), "PC": sb(4, I32), "PF": sb(16),
+    "J16": sb(L), "J12": sb(96), "JG": sb(128), "JA": sb(16), "JB": sb(24), "JC": sb(48), "JD": sb(24),
+    "LQ": sb(16, I32), "L1": sb(16), "L2": sb(16), "L3": sb(16), "L4": sb(16), "L5": sb(16),
+    "LD": sb(24, U16), "LS0": sb(16, U16), "LK": sb(16, U16), "LR": sb(16, U16), "LE": sb(48, U16), "LF": sb(24, U16),
+    "WP": sb(144, BF), "WN": sb(144, BF), "ID": sb(128, BF), "NI": sb(128, BF), "IDF": sb(128),
+    "GO": sb(128, BF), "ONB": sb(128, BF), "ONF": sb(128),
+    "DG": sb(L), "R0": sb(L), "R2": sb(L), "TIE": sb(384), "KR": sb(96), "RZ": sb(96), "RM": sb(96, BF),
+    "MT": sb(128, BF), "ZS": sb(128), "NG": sb(16, BF), "AD": sb(L, BF), "CM": sb(L, BF), "DU": sb(96), "DM": sb(96),
+    "KI": sb(16, I32), "KA": sb(16, I32), "KU": sb(16, U16), "SE": sb(L), "SC": sb(L), "CN": sb(L), "S3": sb(L),
+    "Q1": sb(16), "QM": sb(16), "QU": sb(16, U16), "QC": sb(16), "Q6": sb(16), "QR": sb(L),
+    "DQ": sb(L, BF), "EQ": sb(L), "S2": sb(L), "F1": sb(16), "F2": sb(16), "G1": sb(16), "G2": sb(16),
+    "SA": sb(24, U16), "SB": sb(24, U16), "HH": sb(L, BF), "RV": sb(16, I32), "RVB": sb(16, BF),
+    "BT": sb(128, BF), "BS": sb(4), "BP": sb(128), "PZ": ("psum", [128, 1024], F32),
+}
+PSUM = ("PK", "PZ", "PD", "PT", "PM", "PX0", "PX1")
+for _b in PSUM:
+    SCRATCH.setdefault(_b, ("psum", [128, 512], F32))
+for _t in range(NV):
+    SCRATCH.update({"RB%d" % _t: sb(RBW), "ZR%d" % _t: sb(4 * L, BF), "ZP%d" % _t: sb(L, BF), "ZN%d" % _t: sb(L, BF), "MS%d" % _t: sb(36)})
+TAGS = ("ea", "eb", "ep", "mc", "mz", "mp")
+SEMAPHORES = ["qv", "qs", "qt", "qg", "sent", "dmem", "dplc", "dz", "dtb", "dnx", "dtc", "oyx", "oyz", "oyc", "oyh"] + [
+    "%s%d" % (k, t) for t in range(NV) for k in TAGS]
+
+
+def R(name, lo, hi, step=1, p=None):
+    return (name, lo, hi, step, p)
+
+
+def messages(T, p, t):
+    n = len(T.cores)
+    nxt, mate = (p + 1) % n, p ^ 3
+    rb, rows, zn = "RB%d" % t, R("RB%d" % t, UH - 12, UF - 12), R("ZN%d" % t, 0, L)
+    if t == NV - 1:
+        return {"eb": (rows, R(rb, UF, UN), mate, 0), "mz": (zn, R("ZP%d" % t, 0, L), mate, 0)}
+    nb = "RB%d" % (t + 1)
+    m = {"ea": (R(rb, U0, UH - 12), R(nb, U0 + 12, UH), nxt, 1), "eb": (rows, R(nb, UH, UF), nxt, 0),
+         "mz": (zn, R("ZR%d" % (t + 1), 0, L), nxt, 0), "mc": (R("MS%d" % t, 0, 36), R(nb, 0, 36), nxt, 1)}
+    user = (mate + 1) % n
+    if user != p:
+        m["ep"] = (rows, R(nb, UP, RBW), user, 0)
+        m["mp"] = (zn, R("ZP%d" % t, 0, L), user, 0)
+    return m
+
+
+def first_hop(T, topo, src, dst, h):
+    if topo.may_write(src, dst):
+        return dst
+    able = [c for c in topo.cores_of(src) if c != src and T.rank_of(c) is None and topo.may_write(c, dst)]
+    able.sort(key=lambda c: (topo.die(c) != topo.die(src), c))
+    return able[h % len(able)]
+
+
+def helper_program(g, core, T, topo):
+    sent = 0
+    for t in range(NV):
+        for tag in TAGS:
+            for p, src in enumerate(T.cores):
+                m = messages(T, p, t).get(tag)
+                if m is None or first_hop(T, topo, src, T.cores[m[2]], m[3]) != core:
+                    continue
+                dst = T.cores[m[2]]
+                sem = T.sem["%s%d" % (tag, t)]
+                piece = T[m[1][0]][:, m[1][1]:m[1][2]]
+                g.wait_ge(sem, len(topo.engines(src, core)))
+                rid, pid = topo.addr(dst, core)
+                g.remote_dma(piece, piece, sem, T.sem.sent, pid, rid, topo.mask(core, dst))
+                sent += len(topo.engines(core, dst))
+    if sent:
+        g.wait_ge(T.sem.sent, sent)
+
+
+def emit(g, T, ops):
+    eng = {"v": g.vector, "s": g.scalar, "t": g.tensor, "g": g, "y": g.sync}
+    hist, deps, need = {}, [], set()
+    for i, (q, fn, rd, wr, sem) in enumerate(ops):
+        d = set()
+        for piece, writes in [(r, False) for r in rd] + [(r, True) for r in wr]:
+            whole = piece[0] in PSUM
+            for j, lo, hi, w, st in hist.get(piece[0], []):
+                if not whole and (hi <= piece[1] or piece[2] <= lo or (st == piece[3] and (lo - piece[1]) % st)):
+                    continue
+                same = ops[j][0] == q and ops[j][4] is None and sem is None
+                if not (same and q == "t") and (writes or w or (whole and not same)):
+                    d.add(j)
+        for piece, writes in [(r, False) for r in rd] + [(r, True) for r in wr]:
+            h = hist.setdefault(piece[0], [])
+            if writes:
+                h[:] = [e for e in h if not (piece[3] == 1 and piece[4] is None and piece[1] <= e[1] and e[2] <= piece[2] and e[0] in d)]
+            h.append((i, piece[1], piece[2], writes, piece[3]))
+        last = {}
+        for j in d:
+            if ops[j][4] is None:
+                last[ops[j][0]] = max(last.get(ops[j][0], -1), j)
+            else:
+                last[j] = j
+        deps.append(sorted(last.values()))
+    seen = {q: {} for q in eng}
+    kept = []
+    for i, (q, fn, rd, wr, sem) in enumerate(ops):
+        k = []
+        for j in deps[i]:
+            key = ops[j][0] if ops[j][4] is None else ops[j][4][0]
+            if q != "x" and seen[q].get(key, -1) < j:
+                seen[q][key] = j
+                k.append(j)
+                need.add(j)
+        kept.append(k)
+    count, mark, total = {}, {}, {}
+    for i, (q, fn, rd, wr, sem) in enumerate(ops):
+        if sem is not None:
+            total[sem[0]] = sem[1]
+            mark[i] = sem
+        elif i in need:
+            count[q] = count.get(q, 0) + 1
+            mark[i] = ("q" + q, count[q])
+            total["q" + q] = count[q]
+    for i, (q, fn, rd, wr, sem) in enumerate(ops):
+        if q == "x":
+            continue
+        for j in kept[i]:
+            eng[q].wait_ge(T.sem[mark[j][0]], mark[j][1])
+        ins = fn()
+        if sem is None and i in need:
+            ins.then_inc(T.sem["q" + q], 1)
+    for name in sorted(total):
+        g.wait_ge(T.sem[name], total[name])
+
+
+def rank_program(g, core, T, topo):
+    rank = T.rank_of(core)
+    if rank is None:
+        helper_program(g, core, T, topo)
+        return
+    n = len(T.cores)
+    ops = []
+    sent = [0]
+    V, S, PE = g.vector, g.scalar, g.tensor
+
+    def ap(r):
+        if r[0] == "ind":
+            return ap(r[1]).indirect(ap(r[2]))
+        ps = slice(None) if r[4] is None else slice(*r[4])
+        return T[r[0]][ps, r[1]:r[2]] if r[3] == 1 else T[r[0]][ps, r[1]:r[2]:r[3]]
+
+    def parts(*rs):
+        out = []
+        for r in rs:
+            if isinstance(r, tuple):
+                out += [r[1], r[2]] if r[0] == "ind" else [r]
+        return out
+
+    def val(x):
+        return ap(x) if isinstance(x, tuple) else x
+
+    def rec(q, fn, out, *ins):
+        if out[0] == "ind":
+            ops.append((q, fn, parts(out[2], *ins), [out[1]], None))
+        else:
+            ops.append((q, fn, parts(*ins), [out], None))
+
+    def ind(win, off):
+        return ("ind", win, off)
+
+    def cp(out, a):
+        rec("v", lambda: V.tensor_copy(ap(out), ap(a)), out, a)
+
+    def tt(out, a, b, op):
+        rec("v", lambda: V.tensor_tensor(ap(out), ap(a), ap(b), op), out, a, b)
+
+    def ts(out, a, s1, op0, s2=None, op1=None):
+        if op1 is None:
+            rec("v", lambda: V.tensor_scalar(ap(out), ap(a), val(s1), None, op0), out, a, s1)
+        else:
+            rec("v", lambda: V.tensor_scalar(ap(out), ap(a), val(s1), val(s2), op0, op1), out, a, s1, s2)
+
+    def fill(out, c):
+        rec("v", lambda: V.memset(ap(out), c), out)
+
+    def scan(out, d0, d1):
+        rec("v", lambda: V.tensor_tensor_scan(ap(out), ap(d0), ap(d1), 0.0, ALU.mult, ALU.add), out, d0, d1)
+
+    def turn(a, b):
+        rec("v", lambda: V.transpose(T.TO[:, a:b], T.TI[:, a:b]), R("TO", a, b), R("TI", a, b))
+
+    def act(out, a, func, bias=0.0, scale=1.0):
+        rec("s", lambda: S.activation(ap(out), ap(a), func, bias=val(bias), scale=scale), out, a, bias)
+
+    def mm(out, lhs, rhs, start, stop):
+        rec("t", lambda: PE.matmul(ap(out), ap(lhs), ap(rhs), start, stop), out, lhs, rhs)
+
+    def iota(out, pattern, base=0, cm=0):
+        if SCRATCH[out[0]][2] == I32:
+            rec("g", lambda: g.iota(ap(out), pattern, base, cm), out)
+        else:
+            rec("g", lambda: g.iota(ap(out), pattern, base, cm, allow_small_or_imprecise_dtypes=True), out)
+
+    def gcopy(out, a):
+        rec("g", lambda: g.affine_select(ap(out), ap(a), [[0, a[2] - a[1]]], ALU.is_ge, 0.0, 0, 0), out, a)
+
+    def dma(q, out, a, rd, wr, sem, cnt=16):
+        e = g.sync if q == "y" else g.scalar
+        ops.append((q, lambda: e.dma_start(out, a).then_inc(T.sem[sem], 16), rd, wr, (sem, cnt)))
+
+    def send(tag, t):
+        m = messages(T, rank, t).get(tag)
+        if m is None:
+            return
+        dst = first_hop(T, topo, core, T.cores[m[2]], m[3])
+        rid, pid = topo.addr(dst, core)
+        sent[0] += len(topo.engines(core, dst))
+        ops.append(("g", lambda: g.remote_dma(ap(m[1]), ap(m[0]), T.sem["%s%d" % (tag, t)], T.sem.sent, pid, rid, topo.mask(core, dst)),
+                    [m[0]], [], ("sent", sent[0])))
+
+    def arrive(tag, t):
+        for p in range(n):
+            m = messages(T, p, t).get(tag)
+            if m is not None and m[2] == rank:
+                hop = first_hop(T, topo, T.cores[p], core, m[3])
+                ops.append(("x", None, [], [m[1]], ("%s%d" % (tag, t), len(topo.engines(T.cores[p] if hop == core else hop, core)))))
+
+    def col(name, j, p=None):
+        return R(name, j, j + 1, 1, p)
+
+    def full(name, w, p=None):
+        return R(name, 0, w, 1, p)
+
+    P12, P13, P1 = (0, 12), (0, 13), (0, 1)
+    PP, IL, P31, GB, G0, GB15, D2, TH, BO, BP, I12, TMP = [col("PF", j) for j in range(12)]
+
+    fill(R("HC", L, 2 * L), 0)
+    dma("y", T.HC[:, 0:L], T.mem[:], [], [R("HC", 0, L)], "dmem")
+    dma("s", T.ZR0[:, 0:L], T.zt[:], [], [R("ZR0", 0, L)], "dz")
+    dma("y", T.HC[0:128:16, L:2 * L], T.plc[:], [], [R("HC", L, 2 * L)], "dplc")
+    dma("y", T.TB[:, T1:T2], T.xt[:], [], [R("TB", T1, T2)], "dtb")
+    for i in range(16):
+        dma("y", T.NX[i:128:16, :], T.nxt[:], [], [R("NX", 0, W)] if i == 15 else [], "dnx", 256)
+    dma("y", T.TB[:, T2:T2 + W], T.xt[:], [], [R("TB", T2, T2 + W)], "dtc")
+
+    iota(col("PC", 0), [[0, 1]], 0, 1)
+    iota(full("JA", 14), [[16, 14]])
+    iota(full("JB", 24), [[16, 12], [0, 2]])
+    iota(R("IW", 0, 144), [[1, 144]])
+    iota(full("J12", 96, (0, 16)), [[0, 8], [1, 12]])
+    iota(full("J16", L), [[0, 12], [1, 16]])
+    iota(R("TIE", 0, 192, 1, P1), [[608, 2], [4108, 8], [1, 12]])
+    iota(R("TIE", 192, 384, 1, P1), [[608, 2], [4108, 8], [1, 12]], 8 * 4096 + 192)
+    fill(full("ONF", 128, P1), 1.0)
+    ts(col("PC", 1), col("PC", 0), 15, ALU.bitwise_and)
+    ts(col("PC", 2), col("PC", 0), 31, ALU.bitwise_and)
+    fill(full("NG", 16), -192.0)
+    cp(full("PF", 3), full("PC", 3))
+    fill(full("KR", 96, P1), 1024.0)
+    ts(full("L1", 14), full("JA", 14), IL, ALU.add)
+    ts(full("LD", 24), full("JB", 24), IL, ALU.add)
+    ts(GB, PP, IL, ALU.subtract)
+    ts(full("LQ", 14), full("L1", 14), -5.5, ALU.add, 1.0 / 12, ALU.mult)
+    ts(G0, P31, IL, ALU.subtract)
+    ts(GB15, GB, 15.0, ALU.add)
+    ts(full("L2", 14), full("LQ", 14), -12.0, ALU.mult)
+    ts(full("L3", 14), full("LQ", 14), 2.0, ALU.is_lt, 386.0, ALU.mult)
+    ts(D2, IL, float(W), ALU.add)
+    tt(full("L2", 14), full("L2", 14), full("L1", 14), ALU.add)
+    tt(full("L3", 14), full("L3", 14), full("LQ", 14), ALU.max)
+    ts(I12, PP, 12.0, ALU.is_equal)
+    ts(full("L4", 14), full("L2", 14), 32.0, ALU.mult, G0, ALU.add)
+    cp(R("LK", 0, 6), full("L2", 6))
+    ts(R("LK", 6, 12), full("L2", 6), 12.0, ALU.add)
+    tt(full("L5", 14), full("L4", 14), full("L3", 14), ALU.add)
+    ts(full("ID", 128), R("IW", 0, 128), PP, ALU.is_equal)
+    ts(full("LS0", 14), full("L5", 14), -2.0, ALU.add)
+    ts(full("WP", 144), R("IW", 0, 144), GB15, ALU.is_equal, 2048.0, ALU.mult)
+    ts(full("WN", 144), R("IW", 0, 144), GB15, ALU.is_equal, -1024.0, ALU.mult)
+    ts(full("WI", L), R("HC", 0, L), 1, ALU.bitwise_and)
+    cp(R("UC", L, 2 * L), R("HC", L, 2 * L))
+    act(R("TI", 384, 768), ind(R("UC", L, 2 * L), R("LD", 0, 24)), ACT.Identity)
+    ts(full("WF", L), full("WI", L), -(2 * W + 1.5), ALU.mult)
+    ts(full("RZ", 96, P12), full("J12", 96, P12), col("PF", 0, P12), ALU.is_equal, 0.5, ALU.mult)
+    tt(full("WG", L), full("WF", L), R("HC", 0, L), ALU.add)
+    act(R("TI", 0, 384), ind(full("WG", L), R("LD", 0, 24)), ACT.Abs, scale=0.5)
+    turn(384, 768)
+    ts(full("DG", L), full("J16", L), IL, ALU.is_equal)
+    turn(0, 384)
+    cp(full("LR", 12), R("IW", 0, 12))
+    cp(R("RB0", 0, 224), ind(full("TO", 768), full("LS0", 14)))
+
+    def later_iotas():
+        iota(full("JC", 48), [[0, 2], [1, 12], [0, 2]])
+        iota(full("JD", 24), [[32, 24]])
+        iota(full("JG", 128), [[16, 8], [0, 16]])
+        for a in range(144, W, 976):
+            iota(R("IW", a, a + 976), [[1, 976]], a)
+
+    def spare(t):
+        if t == 0:
+            return [lambda: ts(full("R0", L), full("J16", L), 1.0, ALU.min),
+                    lambda: fill(full("ONB", 128), 1.0),
+                    lambda: ts(full("R2", L), full("R0", L), 2.0, ALU.mult),
+                    lambda: ts(full("NI", 128), R("IW", 0, 128), PP, ALU.is_equal, -1.0, ALU.mult),
+                    lambda: scan(full("S2", L), full("R2", L), full("DG", L)),
+                    lambda: ts(full("FM", 96, P13), full("J12", 96, P13), col("PF", 0, P13), ALU.is_equal, col("PF", 10, P13), ALU.max),
+                    lambda: ts(TH, col("S2", 15), 2.0, ALU.mult),
+                    lambda: ts(full("IDF", 128), R("IW", 0, 128), PP, ALU.is_equal),
+                    lambda: fill(full("MT", 128, (0, 16)), 1.0),
+                    lambda: ts(full("RM", 96, P13), full("FM", 96, P13), 0.5, ALU.mult)]
+        if t == 1:
+            return [lambda: ts(TMP, IL, 0.0, ALU.is_equal, 300.0, ALU.mult),
+                    lambda: ts(BO, IL, 12.0, ALU.mult, -12.0, ALU.add),
+                    lambda: ts(BP, IL, 8.0, ALU.is_ge, 108.0, ALU.mult),
+                    lambda: ts(full("GO", 128), full("JG", 128), GB, ALU.is_equal),
+                    lambda: ts(BO, BO, TMP, ALU.add),
+                    lambda: ts(full("LF", 24), full("JD", 24), P31, ALU.add),
+                    lambda: ts(R("LE", 0, 24), R("JC", 0, 24), BO, ALU.add),
+                    lambda: ts(R("LE", 24, 48), R("JC", 24, 48), BO, ALU.add, BP, ALU.add)]
+        if t == NV - 1:
+            u = R("RB3", U0, UN)
+            return [lambda: ts(full("WI", 288), u, 4.0, ALU.mult),
+                    lambda: ts(full("WJ", 288), full("WI", 288), 1, ALU.bitwise_and),
+                    lambda: ts(full("WF", 288), full("WJ", 288), -(W + 0.75), ALU.mult)]
+        return []
+
+    def open_keys(t):
+        mm(R("PK", 0, 384), full("ONF", 128, P1), full("TIE", 384, P1), True, False)
+        if t > 0:
+            for a in (96, 288):
+                mm(R("PK", a, a + 96), full("BP", 128, P1), full("KR", 96, P1), False, False)
+
+    open_keys(0)
+    for t in range(NV):
+        rb, zr, zn, ms = "RB%d" % t, "ZR%d" % t, "ZN%d" % t, "MS%d" % t
+        z = R(zr, 0, L)
+        last = t == NV - 1
+        win = R("TB", T1, T2 if t == 0 else T2 + W)
+        own_partner = t > 0 and (((rank - 1) % n) ^ 3) == rank
+        zp = R("ZN%d" % (t - 1), 0, L) if own_partner else R("ZP%d" % max(t - 1, 0), 0, L)
+
+        def offsets(h, kind):
+            a = 192 * h + 96 * kind
+            tt(R("OF", a, a + 96), ind(R(rb, 0, U0 if kind else C2), R("LK", 6 * kind, 6 * kind + 6)), R(rb, U0 + 96 * h, UH + 96 * h),
+               ALU.subtract if kind else ALU.add)
+
+        def lists(*pieces):
+            if t == 0:
+                for a, b in pieces:
+                    ts(R("OT", a, b), R("OF", a, b), float(W), ALU.is_ge, float(W), ALU.mult)
+                for a, b in pieces:
+                    tt(R("OM", a, b), R("OF", a, b), R("OT", a, b), ALU.subtract)
+            for a, b in pieces:
+                cp(R("OU", a, b), R("OM" if t == 0 else "OF", a, b))
+
+        def g_a(a, b):
+            tt(R("XB", L * a, L * b), ind(win, R("OU", 12 * a, 12 * b)), R(zr, 0, L * (b - a)), ALU.subtract)
+
+        def abs_a(a, b):
+            act(R("EB", L * a, L * b), R("XB", L * a, L * b), ACT.Abs, scale=0.5)
+
+        def g_b(a, b):
+            act(R("XB", L * a, L * b), ind(win, R("OU", 12 * a, 12 * b)), ACT.Identity)
+
+        def max_b(a, b):
+            tt(R("EB", L * a, L * b), R("XB", L * a, L * b), R("PZ", 0, L * (b - a)), ALU.max)
+
+        def sums(buf, a, b, stop=False):
+            for i in range(16):
+                mm(R("PK", 12 * a, 12 * b), R("WP" if buf == "EB" else "WN", 15 - i, 143 - i), R(buf, L * a + i, L * b, 16),
+                   False, stop and i == 15)
+
+        def turned(src, base):
+            for i in range(16):
+                mm(R("PT", base + i, base + 128, 16, P12), R(src[0], i, L, 16), R("WP", 15, 143, 16), True, True)
+
+        if t > 0:
+            for tag in ("mc", "mz", "mp"):
+                arrive(tag, t - 1)
+            offsets(0, 0)
+            offsets(0, 1)
+            lists((0, 96), (96, 192))
+        else:
+            offsets(0, 0)
+            ts(R(rb, C2, U0), R(rb, C0, C2), W + 0.25, ALU.add)
+            ts(R("OT", 0, 96), R("OF", 0, 96), float(W), ALU.is_ge, float(W), ALU.mult)
+            offsets(0, 1)
+            tt(R("OM", 0, 96), R("OF", 0, 96), R("OT", 0, 96), ALU.subtract)
+            ts(R("OT", 96, 192), R("OF", 96, 192), float(W), ALU.is_ge, float(W), ALU.mult)
+            cp(R("OU", 0, 96), R("OM", 0, 96))
+            tt(R("OM", 96, 192), R("OF", 96, 192), R("OT", 96, 192), ALU.subtract)
+            cp(R("OU", 96, 192), R("OM", 96, 192))
+        gcopy(R(zr, L, 2 * L), z)
+        gcopy(R(zr, 2 * L, 4 * L), R(zr, 0, 2 * L))
+        if t > 0:
+            mm(R("PD", 0, L), full("ID", 128), z, True, False)
+            mm(R("PD", 0, L), full("NI", 128), zp, False, True)
+        for a, b in ((0, 192), (192, 384), (384, 512), (512, 576), (576, 768)):
+            mm(R("PZ", a, b), full("ID", 128), R(zr, a % L, a % L + b - a), True, True)
+        turned(z, 128)
+        g_b(0, 4)
+        if t > 0:
+            cp(R("XB", L * 12, L * 16), ind(win, R("OU", 144, 192)))
+            act(full("AD", L), R("PD", 0, L), ACT.Abs)
+            act(full("ZS", 128, P12), R("PT", 128, 256, 1, P12), ACT.Identity)
+            act(full("CM", L), full("AD", L), ACT.Sign, bias=12.5, scale=-1.0)
+            for j in range(2):
+                mm(R("PX%d" % j, 0, 384), full("ID", 128), R("XB", L * (12 + 2 * j), L * (14 + 2 * j)), True, False)
+                for i in range(2):
+                    mm(R("PX%d" % j, L * i, L * i + L), full("NI", 128), z, False, i == 1)
+                if j == 0:
+                    turned(full("CM", L), 0)
+            act(R("EB", L * 12, L * 14), R("PX0", 0, 384), ACT.Abs, scale=0.5)
+            act(full("MT", 128, P12), R("PT", 0, 128, 1, P12), ACT.Sign, bias=-2048.0)
+            mm(R("PM", 0, 96), full("MT", 128, P13), full("RM", 96, P13), True, True)
+            act(R("EB", L * 14, L * 16), R("PX1", 0, 384), ACT.Abs, scale=0.5)
+            send("ea", t)
+        else:
+            g_a(12, 16)
+            act(full("ZS", 128, P12), R("PT", 128, 256, 1, P12), ACT.Identity)
+            abs_a(12, 16)
+            send("ea", t)
+            send("eb", t)
+            send("ep", t)
+            later_iotas()
+        for a in (96, 288):
+            mm(R("PK", a, a + 96), full("ZS", 128, P12), full("RZ", 96, P12), False, False)
+        max_b(0, 4)
+        g_b(4, 8)
+        if t > 0:
+            g_a(10, 12)
+            tt(full("DM", 96), full("DU", 96), R("PM", 0, 96), ALU.mult)
+            g_a(9, 10)
+            tt(R(rb, UH, UF), R(rb, UH, UF), full("DM", 96), ALU.add)
+            g_a(8, 9)
+            send("eb", t)
+            send("ep", t)
+        else:
+            g_a(8, 12)
+        offsets(1, 0)
+        offsets(1, 1)
+        lists((192, 288), (288, 384))
+        sums("XB", 0, 8)
+        abs_a(8, 12)
+        max_b(4, 8)
+        g_b(16, 20)
+        sums("EB", 0, 16)
+        g_a(28, 32)
+        sums("XB", 16, 20)
+        g_b(20, 24)
+        max_b(16, 20)
+        sums("EB", 16, 20)
+        sums("XB", 20, 24)
+        abs_a(28, 32)
+        g_a(24, 28)
+        sums("EB", 28, 32)
+        abs_a(24, 28)
+        max_b(20, 24)
+        sums("EB", 20, 28, True)
+        if last:
+            arrive("eb", t)
+        extra = spare(t)
+        for f in extra[:5 if t == 0 else 3]:
+            f()
+        extra = extra[5 if t == 0 else 3:]
+
+        def idle():
+            if extra:
+                extra.pop(0)()
+
+        if last:
+            mm(R("PM", 0, 288), full("IDF", 128), R(rb, U0, UN), True, False)
+            mm(R("PM", 0, 288), full("IDF", 128), full("WF", 288), False, True)
+            act(full("MM", 288), R("PM", 0, 288), ACT.Abs, scale=2.0)
+
+        for i in range(12):
+            rec("v", lambda i=i: V.tensor_reduce(T.KI[:, i:i + 1], T.PK[:, i:384:12], AxisListType.X, ALU.min), col("KI", i), R("PK", 0, 384))
+        idle()
+        ts(full("KA", 12), full("KI", 12), 511, ALU.bitwise_and)
+        if not last:
+            ts(full("RV", 12), full("KI", 12), 512, ALU.bitwise_and)
+        cp(full("KU", 12), full("KA", 12))
+        if not last:
+            ts(full("RVB", 12), full("RV", 12), 1.0, ALU.is_ge)
+            for i in range(12):
+                mm(R("PT", 0, 128, 1, P1), col("RVB", i), full("ONB", 128), i == 0, i == 11)
+            act(full("BT", 128, P1), R("PT", 0, 128, 1, P1), ACT.Identity, bias=192.0 - 31.0 / 64, scale=1.0 / 32)
+            act(col("BS", 0, P1), R("PT", 0, 1, 1, P1), ACT.Identity, bias=32.0 * 192)
+            act(full("BP", 128, P1), full("BT", 128, P1), ACT.Identity, bias=col("BS", 0, P1), scale=-32.0)
+            open_keys(t + 1)
+        tt(full("SE", L), ind(full("OF", 384), full("KU", 12)), full("DG", L), ALU.mult)
+        idle()
+        scan(full("SC", L), full("R0", L), full("SE", L))
+        qv = R("SC", 15, L, 16)
+        ts(full("Q1", 12), qv, float(W), ALU.is_ge, float(W), ALU.mult)
+        un = R(rb, UN, UN + 12) if last else R(ms, 24, 36)
+        tt(un, qv, R(rb, C0, C2), ALU.subtract)
+        tt(full("QM", 12), qv, full("Q1", 12), ALU.subtract)
+        if last:
+            ts(R("WI", 288, 300), un, 4.0, ALU.mult)
+        idle()
+        cp(full("QU", 12), full("QM", 12))
+        if last:
+            ts(R("WJ", 288, 300), R("WI", 288, 300), 1, ALU.bitwise_and)
+        if not last:
+            tt(full("CN", L), ind(full("NX", W), full("QU", 12)), full("DG", L), ALU.mult)
+            cp(full("QC", 12), full("QU", 12))
+            scan(full("S3", L), full("R0", L), full("CN", L))
+            ts(full("Q6", 12), full("QC", 12), 16.0, ALU.add)
+            cp(R(ms, 0, 12), R("S3", 15, L, 16))
+            act(R(ms, 12, 24), R("S3", 15, L, 16), ACT.Identity, bias=W + 0.25)
+            send("mc", t)
+            act(full("QR", L), ind(full("QC", 12), full("LR", 12)), ACT.Identity)
+        tt(full("DQ", L), ind(R("TB", T1, T2), full("QU", 12)), z, ALU.subtract)
+        act(full(zn, L), full("DQ", L), ACT.Abs)
+        send("mz", t)
+        send("mp", t)
+        if last:
+            cp(full("QC", 12), full("QU", 12))
+            act(full("QR", L), ind(full("QC", 12), full("LR", 12)), ACT.Identity)
+            ts(R("WF", 288, 300), R("WJ", 288, 300), -(W + 0.75), ALU.mult)
+            dma("y", T.yz[:], T[zn][:], [full(zn, L)], [], "oyz")
+        mm(R("PD", 0, L), full("ID", 128), full("DQ", L), True, False)
+        mm(R("PD", 0, L), full("ID", 128), z, False, False)
+        mm(R("PD", 0, L), full("ID", 128), z, False, True)
+        act(full("HH", L), R("PD", 0, L), ACT.Identity, bias=191.75, scale=0.5)
+        if last:
+            tt(R("WG", 288, 300), R("WF", 288, 300), un, ALU.add)
+            act(R("MM", 288, 300), R("WG", 288, 300), ACT.Abs, scale=2.0)
+            act(full("TI", 768), ind(full("MM", 300), full("LE", 48)), ACT.Identity)
+        tt(full("EQ", L), ind(full("IW", W), full("QU", 12)), full("QR", L), ALU.is_equal)
+        idle()
+        scan(full("S2", L), full("R2", L), full("EQ", L))
+        idle()
+        if not last:
+            for tag in ("ea", "eb", "ep"):
+                arrive(tag, t)
+            mine = ((rank ^ 3) + 1) % n == rank
+            act(full("DM", 96), R("RB%d" % (t + 1), UH, UF), ACT.Identity, scale=-1.0)
+            mm(R("PM", 0, 96), full("IDF", 128), R(rb, UH - 12, UF - 12) if mine else R("RB%d" % (t + 1), UP, RBW), True, False)
+            mm(R("PM", 0, 96), full("IDF", 128), full("DM", 96), False, True)
+            act(full("DU", 96), R("PM", 0, 96), ACT.Identity)
+        bits = R("S2", 15, L, 16)
+        ts(full("F2", 12), bits, TH, ALU.is_ge, D2, ALU.mult)
+        if not last:
+            ts(full("F1", 12), bits, TH, ALU.is_lt, 8192.0, ALU.mult)
+        tt(full("G2", 12), full("F2", 12), full("QC", 12), ALU.max)
+        if not last:
+            tt(full("G1", 12), full("F1", 12), full("Q6", 12), ALU.min)
+        cp(R("SB", 0, 24, 2), full("G2", 12))
+        if not last:
+            ts(R("SA", 0, 24, 2), full("G1", 12), IL, ALU.max)
+        while extra:
+            idle()
+        for i in range(11, -1, -1):
+            tt(ind(R("TB", T2, TE), col("SB", 2 * i)), R("HH", 16 * i, 16 * i + 16), full("NG", 16), ALU.add)
+            if not last:
+                tt(ind(R("TB", 0, T2), col("SA", 2 * i)), R("HH", 16 * i, 16 * i + 16), full("NG", 16), ALU.add)
+
+    dma("y", T.yx[:], T.TB[:, T2:T2 + W], [R("TB", T2, T2 + W)], [], "oyx")
+    arrive("mz", NV - 1)
+    act(R("PX0", 0, L), full("ZN3", L), ACT.Identity, bias=-12.0)
+    act(R("PX1", 0, L), full("ZN3", L), ACT.Identity, bias=12.0)
+    turn(0, 768)
+    act(full("FO", 384), ind(full("TO", 768), full("LF", 24)), ACT.Identity)
+    act(R("PZ", 0, L), R("FO", 0, L), ACT.Identity)
+    cp(full("CB", L), ind(full("NX", W), full("QU", 12)))
+    dma("y", T.yc[:], T.CB[0:128:16, :], [full("CB", L)], [], "oyc")
+    tt(R("PD", 0, L), R("FO", L, 2 * L), R("FO", 0, L), ALU.subtract)
+    tt(full("AD", L), full("ZP3", L), R("PX0", 0, L), ALU.is_ge)
+    tt(full("CM", L), full("ZP3", L), R("PX1", 0, L), ALU.is_le)
+    mm(R("PT", 0, L), full("GO", 128), full("AD", L), True, False)
+    mm(R("PT", 0, L), full("GO", 128), full("CM", L), False, True)
+    ts(full("FM", L), R("PT", 0, L), 16.0 + 9, ALU.is_ge)
+    tt(full("FN", L), full("FM", L), R("PD", 0, L), ALU.mult)
+    tt(full("FH", L), full("FN", L), R("PZ", 0, L), ALU.add)
+    dma("y", T.yh[:], T.FH[:], [full("FH", L)], [], "oyh")
+    emit(g, T, ops)

@@ -13,7 +13,7 @@ def sb(w, dt=F32):
 
 
 SCRATCH = {
-    "TB": sb(TE, BF), "NX": sb(W, I32), "IW": sb(W), "XB": sb(32 * L, BF), "EB": sb(32 * L, BF),
+    "TB": sb(TE, BF), "NX": sb(2 * W, I32), "QW": sb(16, U16), "IW": sb(2 * W), "QF": sb(16), "Q7": sb(16), "RT": sb(L), "XB": sb(32 * L, BF), "EB": sb(32 * L, BF),
     "HC": sb(384, I32), "UC": sb(384), "TI": sb(768), "TO": sb(768),
     "WI": sb(304, I32), "WJ": sb(304, I32), "WF": sb(304), "WG": sb(304), "MM": sb(304), "FO": sb(384),
     "FM": sb(L), "FN": sb(L), "FH": sb(L), "CB": sb(L),
@@ -37,7 +37,7 @@ for _b in PSUM:
 for _t in range(NV):
     SCRATCH.update({"RB%d" % _t: sb(RBW), "ZR%d" % _t: sb(4 * L, BF), "ZP%d" % _t: sb(L, BF), "ZN%d" % _t: sb(L, BF), "MS%d" % _t: sb(36)})
 TAGS = ("ea", "eb", "ep", "mc", "mz", "mp")
-SEMAPHORES = ["qv", "qs", "qt", "qg", "sent", "dmem", "dplc", "dz", "dtb", "dnx", "dtc", "oyx", "oyz", "oyc", "oyh"] + [
+SEMAPHORES = ["qv", "qs", "qt", "qg", "sent", "dmem", "dplc", "dz", "dtb", "dnx", "dtc", "dny", "oyx", "oyz", "oyc", "oyh"] + [
     "%s%d" % (k, t) for t in range(NV) for k in TAGS]
 
 
@@ -252,7 +252,7 @@ def rank_program(g, core, T, topo):
     dma("y", T.HC[0:128:16, L:2 * L], T.plc[:], [], [R("HC", L, 2 * L)], "dplc")
     dma("y", T.TB[:, T1:T2], T.xt[:], [], [R("TB", T1, T2)], "dtb")
     for i in range(16):
-        dma("y", T.NX[i:128:16, :], T.nxt[:], [], [R("NX", 0, W)] if i == 15 else [], "dnx", 256)
+        dma("y", T.NX[i:128:16, 0:W], T.nxt[:], [], [R("NX", 0, W)] if i == 15 else [], "dnx", 256)
     dma("y", T.TB[:, T2:T2 + W], T.xt[:], [], [R("TB", T2, T2 + W)], "dtc")
 
     iota(col("PC", 0), [[0, 1]], 0, 1)
@@ -313,11 +313,10 @@ def rank_program(g, core, T, topo):
         if t == 0:
             return [lambda: ts(full("R0", L), full("J16", L), 1.0, ALU.min),
                     lambda: fill(full("ONB", 128), 1.0),
-                    lambda: ts(full("R2", L), full("R0", L), 2.0, ALU.mult),
+                    lambda: ts(full("RT", L), full("DG", L), 2.0 ** 19 - 1, ALU.mult, 1.0, ALU.add),
                     lambda: ts(full("NI", 128), R("IW", 0, 128), PP, ALU.is_equal, -1.0, ALU.mult),
-                    lambda: scan(full("S2", L), full("R2", L), full("DG", L)),
+                    lambda: tt(full("R2", L), full("R0", L), full("RT", L), ALU.mult),
                     lambda: ts(full("FM", 96, P13), full("J12", 96, P13), col("PF", 0, P13), ALU.is_equal, col("PF", 10, P13), ALU.max),
-                    lambda: ts(TH, col("S2", 15), 2.0, ALU.mult),
                     lambda: ts(full("IDF", 128), R("IW", 0, 128), PP, ALU.is_equal),
                     lambda: fill(full("MT", 128, (0, 16)), 1.0),
                     lambda: ts(full("RM", 96, P13), full("FM", 96, P13), 0.5, ALU.mult)]
@@ -390,6 +389,8 @@ def rank_program(g, core, T, topo):
         if t > 0:
             for tag in ("mc", "mz", "mp"):
                 arrive(tag, t - 1)
+            if t == 1:
+                dma("y", T.NX[:, W:2 * W], T.NX[:, 0:W], [R("NX", 0, W), R(rb, C0, C2), z], [R("NX", W, 2 * W)], "dny")
             offsets(0, 0)
             offsets(0, 1)
             lists((0, 96), (96, 192))
@@ -442,10 +443,10 @@ def rank_program(g, core, T, topo):
         g_b(4, 8)
         if t > 0:
             g_a(10, 12)
-            tt(full("DM", 96), full("DU", 96), R("PM", 0, 96), ALU.mult)
             g_a(9, 10)
-            tt(R(rb, UH, UF), R(rb, UH, UF), full("DM", 96), ALU.add)
+            tt(full("DM", 96), full("DU", 96), R("PM", 0, 96), ALU.mult)
             g_a(8, 9)
+            tt(R(rb, UH, UF), R(rb, UH, UF), full("DM", 96), ALU.add)
             send("eb", t)
             send("ep", t)
         else:
@@ -473,18 +474,17 @@ def rank_program(g, core, T, topo):
         if last:
             arrive("eb", t)
         extra = spare(t)
-        for f in extra[:5 if t == 0 else 3]:
+        early = (5, 3, 0, 0)[t]
+        for f in extra[:early]:
             f()
-        extra = extra[5 if t == 0 else 3:]
+        extra = extra[early:]
 
         def idle():
             if extra:
                 extra.pop(0)()
 
-        if last:
-            mm(R("PM", 0, 288), full("IDF", 128), R(rb, U0, UN), True, False)
-            mm(R("PM", 0, 288), full("IDF", 128), full("WF", 288), False, True)
-            act(full("MM", 288), R("PM", 0, 288), ACT.Abs, scale=2.0)
+        if t == 1:
+            act(R("IW", W + 2048, 2 * W), R("IW", 2048, W), ACT.Identity)
 
         for i in range(12):
             rec("v", lambda i=i: V.tensor_reduce(T.KI[:, i:i + 1], T.PK[:, i:384:12], AxisListType.X, ALU.min), col("KI", i), R("PK", 0, 384))
@@ -492,6 +492,8 @@ def rank_program(g, core, T, topo):
         ts(full("KA", 12), full("KI", 12), 511, ALU.bitwise_and)
         if not last:
             ts(full("RV", 12), full("KI", 12), 512, ALU.bitwise_and)
+        else:
+            idle()
         cp(full("KU", 12), full("KA", 12))
         if not last:
             ts(full("RVB", 12), full("RV", 12), 1.0, ALU.is_ge)
@@ -504,35 +506,49 @@ def rank_program(g, core, T, topo):
         tt(full("SE", L), ind(full("OF", 384), full("KU", 12)), full("DG", L), ALU.mult)
         idle()
         scan(full("SC", L), full("R0", L), full("SE", L))
+        if last:
+            mm(R("PM", 0, 288), full("IDF", 128), R(rb, U0, UN), True, False)
+            mm(R("PM", 0, 288), full("IDF", 128), full("WF", 288), False, True)
+            act(full("MM", 288), R("PM", 0, 288), ACT.Abs, scale=2.0)
         qv = R("SC", 15, L, 16)
-        ts(full("Q1", 12), qv, float(W), ALU.is_ge, float(W), ALU.mult)
         un = R(rb, UN, UN + 12) if last else R(ms, 24, 36)
+        if t > 0:
+            cp(full("QW", 12), qv)
+        ts(full("Q1", 12), qv, float(W), ALU.is_ge, float(W), ALU.mult)
         tt(un, qv, R(rb, C0, C2), ALU.subtract)
-        tt(full("QM", 12), qv, full("Q1", 12), ALU.subtract)
-        if last:
-            ts(R("WI", 288, 300), un, 4.0, ALU.mult)
-        idle()
-        cp(full("QU", 12), full("QM", 12))
-        if last:
-            ts(R("WJ", 288, 300), R("WI", 288, 300), 1, ALU.bitwise_and)
+        if t == 0:
+            tt(full("QM", 12), qv, full("Q1", 12), ALU.subtract)
+            idle()
+            cp(full("QU", 12), full("QM", 12))
+        qw = full("QW" if t > 0 else "QU", 12)
         if not last:
-            tt(full("CN", L), ind(full("NX", W), full("QU", 12)), full("DG", L), ALU.mult)
-            cp(full("QC", 12), full("QU", 12))
+            tt(full("CN", L), ind(full("NX", 2 * W if t > 0 else W), qw), full("DG", L), ALU.mult)
+            cp(full("QF" if t > 0 else "QC", 12), qw)
             scan(full("S3", L), full("R0", L), full("CN", L))
-            ts(full("Q6", 12), full("QC", 12), 16.0, ALU.add)
+            if t > 0:
+                tt(full("QC", 12), full("QF", 12), full("Q1", 12), ALU.subtract)
             cp(R(ms, 0, 12), R("S3", 15, L, 16))
             act(R(ms, 12, 24), R("S3", 15, L, 16), ACT.Identity, bias=W + 0.25)
             send("mc", t)
             act(full("QR", L), ind(full("QC", 12), full("LR", 12)), ACT.Identity)
-        tt(full("DQ", L), ind(R("TB", T1, T2), full("QU", 12)), z, ALU.subtract)
+        else:
+            cp(full("QF", 12), qw)
+        tt(full("DQ", L), ind(win, qw), z, ALU.subtract)
+        if last:
+            tt(full("QC", 12), full("QF", 12), full("Q1", 12), ALU.subtract)
+            ts(R("WI", 288, 300), un, 4.0, ALU.mult)
         act(full(zn, L), full("DQ", L), ACT.Abs)
         send("mz", t)
         send("mp", t)
         if last:
-            cp(full("QC", 12), full("QU", 12))
             act(full("QR", L), ind(full("QC", 12), full("LR", 12)), ACT.Identity)
+            ts(R("WJ", 288, 300), R("WI", 288, 300), 1, ALU.bitwise_and)
+            ts(full("Q7", 12), full("QC", 12), 64.0, ALU.mult)
             ts(R("WF", 288, 300), R("WJ", 288, 300), -(W + 0.75), ALU.mult)
             dma("y", T.yz[:], T[zn][:], [full(zn, L)], [], "oyz")
+        else:
+            ts(full("Q7", 12), full("QC", 12), 64.0, ALU.mult)
+            ts(full("Q6", 12), full("QC", 12), 64.0, ALU.mult, 64.0 * 16 + 24, ALU.add)
         mm(R("PD", 0, L), full("ID", 128), full("DQ", L), True, False)
         mm(R("PD", 0, L), full("ID", 128), z, False, False)
         mm(R("PD", 0, L), full("ID", 128), z, False, True)
@@ -541,7 +557,7 @@ def rank_program(g, core, T, topo):
             tt(R("WG", 288, 300), R("WF", 288, 300), un, ALU.add)
             act(R("MM", 288, 300), R("WG", 288, 300), ACT.Abs, scale=2.0)
             act(full("TI", 768), ind(full("MM", 300), full("LE", 48)), ACT.Identity)
-        tt(full("EQ", L), ind(full("IW", W), full("QU", 12)), full("QR", L), ALU.is_equal)
+        tt(full("EQ", L), ind(full("IW", 2 * W if t > 0 else W), qw), full("QR", L), ALU.is_equal)
         idle()
         scan(full("S2", L), full("R2", L), full("EQ", L))
         idle()
@@ -553,33 +569,36 @@ def rank_program(g, core, T, topo):
             mm(R("PM", 0, 96), full("IDF", 128), R(rb, UH - 12, UF - 12) if mine else R("RB%d" % (t + 1), UP, RBW), True, False)
             mm(R("PM", 0, 96), full("IDF", 128), full("DM", 96), False, True)
             act(full("DU", 96), R("PM", 0, 96), ACT.Identity)
+            if t == 0:
+                act(R("IW", W, W + 2048), R("IW", 0, 2048), ACT.Identity)
         bits = R("S2", 15, L, 16)
-        ts(full("F2", 12), bits, TH, ALU.is_ge, D2, ALU.mult)
+        tt(full("G2", 12), full("Q7", 12), bits, ALU.add)
         if not last:
-            ts(full("F1", 12), bits, TH, ALU.is_lt, 8192.0, ALU.mult)
-        tt(full("G2", 12), full("F2", 12), full("QC", 12), ALU.max)
+            tt(full("G1", 12), full("Q6", 12), bits, ALU.subtract)
+        ts(R("SB", 0, 24, 2), full("G2", 12), 1.0 / 64, ALU.mult, D2, ALU.min)
         if not last:
-            tt(full("G1", 12), full("F1", 12), full("Q6", 12), ALU.min)
-        cp(R("SB", 0, 24, 2), full("G2", 12))
-        if not last:
-            ts(R("SA", 0, 24, 2), full("G1", 12), IL, ALU.max)
+            ts(R("SA", 0, 24, 2), full("G1", 12), 1.0 / 64, ALU.mult, IL, ALU.max)
         while extra:
             idle()
         for i in range(11, -1, -1):
             tt(ind(R("TB", T2, TE), col("SB", 2 * i)), R("HH", 16 * i, 16 * i + 16), full("NG", 16), ALU.add)
             if not last:
                 tt(ind(R("TB", 0, T2), col("SA", 2 * i)), R("HH", 16 * i, 16 * i + 16), full("NG", 16), ALU.add)
+            elif i == 11:
+                cp(full("CB", L), ind(full("NX", 2 * W), qw))
+                dma("y", T.yc[:], T.CB[0:128:16, :], [full("CB", L)], [], "oyc")
+            elif 5 <= i < 9:
+                turn(192 * (8 - i), 192 * (9 - i))
+            elif i == 4:
+                act(full("FO", 384), ind(full("TO", 768), full("LF", 24)), ACT.Identity)
+                act(R("PX0", 0, L), full("ZN3", L), ACT.Identity, bias=-12.0)
+                act(R("PX1", 0, L), full("ZN3", L), ACT.Identity, bias=12.0)
+                act(R("PZ", 0, L), R("FO", 0, L), ACT.Identity)
+            elif i == 0:
+                tt(R("PD", 0, L), R("FO", L, 2 * L), R("FO", 0, L), ALU.subtract)
 
     dma("y", T.yx[:], T.TB[:, T2:T2 + W], [R("TB", T2, T2 + W)], [], "oyx")
     arrive("mz", NV - 1)
-    act(R("PX0", 0, L), full("ZN3", L), ACT.Identity, bias=-12.0)
-    act(R("PX1", 0, L), full("ZN3", L), ACT.Identity, bias=12.0)
-    turn(0, 768)
-    act(full("FO", 384), ind(full("TO", 768), full("LF", 24)), ACT.Identity)
-    act(R("PZ", 0, L), R("FO", 0, L), ACT.Identity)
-    cp(full("CB", L), ind(full("NX", W), full("QU", 12)))
-    dma("y", T.yc[:], T.CB[0:128:16, :], [full("CB", L)], [], "oyc")
-    tt(R("PD", 0, L), R("FO", L, 2 * L), R("FO", 0, L), ALU.subtract)
     tt(full("AD", L), full("ZP3", L), R("PX0", 0, L), ALU.is_ge)
     tt(full("CM", L), full("ZP3", L), R("PX1", 0, L), ALU.is_le)
     mm(R("PT", 0, L), full("GO", 128), full("AD", L), True, False)

@@ -5,7 +5,7 @@ ACT = ActivationFunctionType
 W, L, NV = 3072, 192, 4
 F32, BF, I32, U16 = "float32", "bfloat16", "int32", "uint16"
 C0, C2, U0, UH, UF, UN, UP, RBW = 0, 12, 24, 120, 216, 312, 328, 424
-T1, T2, TE = 16, 16 + W, 32 + 2 * W
+T1, T2, TE = 32, 32 + W, 64 + 2 * W
 
 
 def sb(w, dt=F32):
@@ -13,21 +13,21 @@ def sb(w, dt=F32):
 
 
 SCRATCH = {
-    "TB": sb(TE, BF), "NX": sb(2 * W, I32), "QW": sb(16, U16), "IW": sb(2 * W), "QF": sb(16), "Q7": sb(16), "RT": sb(L), "XB": sb(32 * L, BF), "EB": sb(32 * L, BF),
+    "TB": sb(TE, BF), "NX": sb(2 * W, I32), "QW": sb(16, U16), "IW": sb(2 * W), "QF": sb(16), "Q7": sb(16), "RT": sb(384), "JX": sb(384), "QD": sb(24, U16), "XB": sb(32 * L, BF), "EB": sb(32 * L, BF),
     "HC": sb(384, I32), "UC": sb(384), "TI": sb(768), "TO": sb(768),
     "WI": sb(304, I32), "WJ": sb(304, I32), "WF": sb(304), "WG": sb(304), "MM": sb(304), "FO": sb(384),
     "FM": sb(L), "FN": sb(L), "FH": sb(L), "CB": sb(L),
     "OF": sb(384), "OT": sb(384), "OM": sb(384), "OU": sb(384, U16), "PC": sb(4, I32), "PF": sb(16),
     "J16": sb(L), "J12": sb(96), "JG": sb(128), "JA": sb(16), "JB": sb(24), "JC": sb(48), "JD": sb(24),
     "LQ": sb(16, I32), "L1": sb(16), "L2": sb(16), "L3": sb(16), "L4": sb(16), "L5": sb(16),
-    "LD": sb(24, U16), "LS0": sb(16, U16), "LK": sb(16, U16), "LR": sb(16, U16), "LE": sb(48, U16), "LF": sb(24, U16),
+    "LD": sb(24, U16), "LS0": sb(16, U16), "LK": sb(16, U16), "LR": sb(24, U16), "LE": sb(48, U16), "LF": sb(24, U16),
     "WP": sb(144, BF), "WN": sb(144, BF), "ID": sb(128, BF), "NI": sb(128, BF), "IDF": sb(128),
     "GO": sb(128, BF), "ONB": sb(128, BF), "ONF": sb(128),
-    "DG": sb(L), "R0": sb(L), "R2": sb(L), "TIE": sb(384), "KR": sb(96), "RZ": sb(96), "RM": sb(96, BF),
-    "MT": sb(128, BF), "ZS": sb(128), "NG": sb(16, BF), "AD": sb(L, BF), "CM": sb(L, BF), "DU": sb(96), "DM": sb(96),
+    "DG": sb(L), "R0": sb(L), "R2": sb(384), "TIE": sb(384), "KR": sb(96), "RZ": sb(96), "RM": sb(96, BF),
+    "MT": sb(128, BF), "ZS": sb(128), "NG": sb(32, BF), "AD": sb(L, BF), "CM": sb(L, BF), "DU": sb(96), "DM": sb(96),
     "KI": sb(16, I32), "KA": sb(16, I32), "KU": sb(16, U16), "SE": sb(L), "SC": sb(L), "CN": sb(L), "S3": sb(L),
-    "Q1": sb(16), "QM": sb(16), "QU": sb(16, U16), "QC": sb(16), "Q6": sb(16), "QR": sb(L),
-    "DQ": sb(L, BF), "EQ": sb(L), "S2": sb(L), "F1": sb(16), "F2": sb(16), "G1": sb(16), "G2": sb(16),
+    "Q1": sb(16), "QM": sb(16), "QU": sb(16, U16), "QC": sb(16), "Q6": sb(16), "QR": sb(384),
+    "DQ": sb(L, BF), "EQ": sb(384), "S2": sb(384), "G1": sb(16), "G2": sb(16),
     "SA": sb(24, U16), "SB": sb(24, U16), "HH": sb(L, BF), "RV": sb(16, I32), "RVB": sb(16, BF),
     "BT": sb(128, BF), "BS": sb(4), "BP": sb(128), "PZ": ("psum", [128, 1024], F32),
 }
@@ -244,7 +244,7 @@ def rank_program(g, core, T, topo):
         return R(name, 0, w, 1, p)
 
     P12, P13, P1 = (0, 12), (0, 13), (0, 1)
-    PP, IL, P31, GB, G0, GB15, D2, TH, BO, BP, I12, TMP = [col("PF", j) for j in range(12)]
+    PP, IL, P31, GB, G0, GB15, D2, TH, BO, BP, I12, TMP, D3 = [col("PF", j) for j in range(13)]
 
     fill(R("HC", L, 2 * L), 0)
     dma("y", T.HC[:, 0:L], T.mem[:], [], [R("HC", 0, L)], "dmem")
@@ -266,7 +266,7 @@ def rank_program(g, core, T, topo):
     fill(full("ONF", 128, P1), 1.0)
     ts(col("PC", 1), col("PC", 0), 15, ALU.bitwise_and)
     ts(col("PC", 2), col("PC", 0), 31, ALU.bitwise_and)
-    fill(full("NG", 16), -192.0)
+    fill(full("NG", 32), -192.0)
     cp(full("PF", 3), full("PC", 3))
     fill(full("KR", 96, P1), 1024.0)
     ts(full("L1", 14), full("JA", 14), IL, ALU.add)
@@ -284,26 +284,28 @@ def rank_program(g, core, T, topo):
     ts(full("L4", 14), full("L2", 14), 32.0, ALU.mult, G0, ALU.add)
     cp(R("LK", 0, 6), full("L2", 6))
     ts(R("LK", 6, 12), full("L2", 6), 12.0, ALU.add)
-    tt(full("L5", 14), full("L4", 14), full("L3", 14), ALU.add)
-    ts(full("ID", 128), R("IW", 0, 128), PP, ALU.is_equal)
-    ts(full("LS0", 14), full("L5", 14), -2.0, ALU.add)
-    ts(full("WP", 144), R("IW", 0, 144), GB15, ALU.is_equal, 2048.0, ALU.mult)
-    ts(full("WN", 144), R("IW", 0, 144), GB15, ALU.is_equal, -1024.0, ALU.mult)
     ts(full("WI", L), R("HC", 0, L), 1, ALU.bitwise_and)
     cp(R("UC", L, 2 * L), R("HC", L, 2 * L))
+    tt(full("L5", 14), full("L4", 14), full("L3", 14), ALU.add)
     act(R("TI", 384, 768), ind(R("UC", L, 2 * L), R("LD", 0, 24)), ACT.Identity)
     ts(full("WF", L), full("WI", L), -(2 * W + 1.5), ALU.mult)
-    ts(full("RZ", 96, P12), full("J12", 96, P12), col("PF", 0, P12), ALU.is_equal, 0.5, ALU.mult)
+    ts(full("ID", 128), R("IW", 0, 128), PP, ALU.is_equal)
+    ts(full("LS0", 14), full("L5", 14), -2.0, ALU.add)
     tt(full("WG", L), full("WF", L), R("HC", 0, L), ALU.add)
     act(R("TI", 0, 384), ind(full("WG", L), R("LD", 0, 24)), ACT.Abs, scale=0.5)
+    ts(full("WP", 144), R("IW", 0, 144), GB15, ALU.is_equal, 2048.0, ALU.mult)
+    ts(full("WN", 144), R("IW", 0, 144), GB15, ALU.is_equal, -1024.0, ALU.mult)
     turn(384, 768)
+    ts(full("RZ", 96, P12), full("J12", 96, P12), col("PF", 0, P12), ALU.is_equal, 0.5, ALU.mult)
     ts(full("DG", L), full("J16", L), IL, ALU.is_equal)
     turn(0, 384)
-    cp(full("LR", 12), R("IW", 0, 12))
+    ts(TH, IL, 16.0, ALU.add)
+    ts(D3, IL, W + 16.0, ALU.add)
     cp(R("RB0", 0, 224), ind(full("TO", 768), full("LS0", 14)))
 
     def later_iotas():
         iota(full("JC", 48), [[0, 2], [1, 12], [0, 2]])
+        iota(full("JX", 384), [[0, 6], [-16, 2], [1, 32]])
         iota(full("JD", 24), [[32, 24]])
         iota(full("JG", 128), [[16, 8], [0, 16]])
         for a in range(144, W, 976):
@@ -313,9 +315,11 @@ def rank_program(g, core, T, topo):
         if t == 0:
             return [lambda: ts(full("R0", L), full("J16", L), 1.0, ALU.min),
                     lambda: fill(full("ONB", 128), 1.0),
-                    lambda: ts(full("RT", L), full("DG", L), 2.0 ** 19 - 1, ALU.mult, 1.0, ALU.add),
+                    lambda: ts(full("RT", 384), full("JX", 384), IL, ALU.is_equal, 2.0 ** 20 - 1, ALU.mult),
                     lambda: ts(full("NI", 128), R("IW", 0, 128), PP, ALU.is_equal, -1.0, ALU.mult),
-                    lambda: tt(full("R2", L), full("R0", L), full("RT", L), ALU.mult),
+                    lambda: act(full("R2", 384), full("RT", 384), ACT.Identity, bias=1.0),
+                    lambda: cp(full("LR", 24), full("JC", 24)),
+                    lambda: fill(R("R2", 0, 384, 32), 0.0),
                     lambda: ts(full("FM", 96, P13), full("J12", 96, P13), col("PF", 0, P13), ALU.is_equal, col("PF", 10, P13), ALU.max),
                     lambda: ts(full("IDF", 128), R("IW", 0, 128), PP, ALU.is_equal),
                     lambda: fill(full("MT", 128, (0, 16)), 1.0),
@@ -414,33 +418,34 @@ def rank_program(g, core, T, topo):
         turned(z, 128)
         g_b(0, 4)
         if t > 0:
-            cp(R("XB", L * 12, L * 16), ind(win, R("OU", 144, 192)))
+            cp(R("XB", L * 4, L * 8), ind(win, R("OU", 48, 96)))
             act(full("AD", L), R("PD", 0, L), ACT.Abs)
             act(full("ZS", 128, P12), R("PT", 128, 256, 1, P12), ACT.Identity)
             act(full("CM", L), full("AD", L), ACT.Sign, bias=12.5, scale=-1.0)
             for j in range(2):
-                mm(R("PX%d" % j, 0, 384), full("ID", 128), R("XB", L * (12 + 2 * j), L * (14 + 2 * j)), True, False)
+                mm(R("PX%d" % j, 0, 384), full("ID", 128), R("XB", L * (4 + 2 * j), L * (6 + 2 * j)), True, False)
                 for i in range(2):
                     mm(R("PX%d" % j, L * i, L * i + L), full("NI", 128), z, False, i == 1)
                 if j == 0:
                     turned(full("CM", L), 0)
-            act(R("EB", L * 12, L * 14), R("PX0", 0, 384), ACT.Abs, scale=0.5)
+            act(R("EB", L * 4, L * 6), R("PX0", 0, 384), ACT.Abs, scale=0.5)
             act(full("MT", 128, P12), R("PT", 0, 128, 1, P12), ACT.Sign, bias=-2048.0)
             mm(R("PM", 0, 96), full("MT", 128, P13), full("RM", 96, P13), True, True)
-            act(R("EB", L * 14, L * 16), R("PX1", 0, 384), ACT.Abs, scale=0.5)
+            act(R("EB", L * 6, L * 8), R("PX1", 0, 384), ACT.Abs, scale=0.5)
             send("ea", t)
         else:
-            g_a(12, 16)
+            g_a(4, 8)
             act(full("ZS", 128, P12), R("PT", 128, 256, 1, P12), ACT.Identity)
-            abs_a(12, 16)
+            abs_a(4, 8)
             send("ea", t)
             send("eb", t)
             send("ep", t)
             later_iotas()
-        for a in (96, 288):
+        for a in (48, 288):
             mm(R("PK", a, a + 96), full("ZS", 128, P12), full("RZ", 96, P12), False, False)
         max_b(0, 4)
-        g_b(4, 8)
+        sums("XB", 0, 4)
+        g_b(12, 16)
         if t > 0:
             g_a(10, 12)
             g_a(9, 10)
@@ -454,9 +459,9 @@ def rank_program(g, core, T, topo):
         offsets(1, 0)
         offsets(1, 1)
         lists((192, 288), (288, 384))
-        sums("XB", 0, 8)
+        sums("XB", 12, 16)
         abs_a(8, 12)
-        max_b(4, 8)
+        max_b(12, 16)
         g_b(16, 20)
         sums("EB", 0, 16)
         g_a(28, 32)
@@ -521,16 +526,23 @@ def rank_program(g, core, T, topo):
             idle()
             cp(full("QU", 12), full("QM", 12))
         qw = full("QW" if t > 0 else "QU", 12)
+
+        def pairs(r):
+            for i in range(2):
+                cp(R("QD", 2 * r + i, 24, 4), R(qw[0], i, 12, 2))
+
         if not last:
             tt(full("CN", L), ind(full("NX", 2 * W if t > 0 else W), qw), full("DG", L), ALU.mult)
             cp(full("QF" if t > 0 else "QC", 12), qw)
+            pairs(0)
             scan(full("S3", L), full("R0", L), full("CN", L))
             if t > 0:
                 tt(full("QC", 12), full("QF", 12), full("Q1", 12), ALU.subtract)
+            pairs(1)
             cp(R(ms, 0, 12), R("S3", 15, L, 16))
             act(R(ms, 12, 24), R("S3", 15, L, 16), ACT.Identity, bias=W + 0.25)
             send("mc", t)
-            act(full("QR", L), ind(full("QC", 12), full("LR", 12)), ACT.Identity)
+            act(full("QR", 384), ind(full("QC", 12), full("LR", 24)), ACT.Identity)
         else:
             cp(full("QF", 12), qw)
         tt(full("DQ", L), ind(win, qw), z, ALU.subtract)
@@ -541,14 +553,16 @@ def rank_program(g, core, T, topo):
         send("mz", t)
         send("mp", t)
         if last:
-            act(full("QR", L), ind(full("QC", 12), full("LR", 12)), ACT.Identity)
+            act(full("QR", 384), ind(full("QC", 12), full("LR", 24)), ACT.Identity)
+            pairs(0)
+            pairs(1)
             ts(R("WJ", 288, 300), R("WI", 288, 300), 1, ALU.bitwise_and)
-            ts(full("Q7", 12), full("QC", 12), 64.0, ALU.mult)
+            ts(full("Q7", 12), full("QC", 12), 128.0, ALU.mult)
             ts(R("WF", 288, 300), R("WJ", 288, 300), -(W + 0.75), ALU.mult)
             dma("y", T.yz[:], T[zn][:], [full(zn, L)], [], "oyz")
         else:
-            ts(full("Q7", 12), full("QC", 12), 64.0, ALU.mult)
-            ts(full("Q6", 12), full("QC", 12), 64.0, ALU.mult, 64.0 * 16 + 24, ALU.add)
+            ts(full("Q7", 12), full("QC", 12), 128.0, ALU.mult)
+            ts(full("Q6", 12), full("QC", 12), 128.0, ALU.mult, 128.0 * T1 + 48, ALU.add)
         mm(R("PD", 0, L), full("ID", 128), full("DQ", L), True, False)
         mm(R("PD", 0, L), full("ID", 128), z, False, False)
         mm(R("PD", 0, L), full("ID", 128), z, False, True)
@@ -557,9 +571,11 @@ def rank_program(g, core, T, topo):
             tt(R("WG", 288, 300), R("WF", 288, 300), un, ALU.add)
             act(R("MM", 288, 300), R("WG", 288, 300), ACT.Abs, scale=2.0)
             act(full("TI", 768), ind(full("MM", 300), full("LE", 48)), ACT.Identity)
-        tt(full("EQ", L), ind(full("IW", 2 * W if t > 0 else W), qw), full("QR", L), ALU.is_equal)
+            act(R("PX0", 0, L), full("ZN3", L), ACT.Identity, bias=-12.0)
+            act(R("PX1", 0, L), full("ZN3", L), ACT.Identity, bias=12.0)
+        tt(full("EQ", 384), ind(full("IW", 2 * W if t > 0 else W), full("QD", 24)), full("QR", 384), ALU.is_equal)
         idle()
-        scan(full("S2", L), full("R2", L), full("EQ", L))
+        scan(full("S2", 384), full("R2", 384), full("EQ", 384))
         idle()
         if not last:
             for tag in ("ea", "eb", "ep"):
@@ -571,31 +587,28 @@ def rank_program(g, core, T, topo):
             act(full("DU", 96), R("PM", 0, 96), ACT.Identity)
             if t == 0:
                 act(R("IW", W, W + 2048), R("IW", 0, 2048), ACT.Identity)
-        bits = R("S2", 15, L, 16)
+        bits = R("S2", 31, 384, 32)
         tt(full("G2", 12), full("Q7", 12), bits, ALU.add)
         if not last:
             tt(full("G1", 12), full("Q6", 12), bits, ALU.subtract)
-        ts(R("SB", 0, 24, 2), full("G2", 12), 1.0 / 64, ALU.mult, D2, ALU.min)
-        if not last:
-            ts(R("SA", 0, 24, 2), full("G1", 12), 1.0 / 64, ALU.mult, IL, ALU.max)
+        for r in range(2):
+            ts(R("SB", r, 12, 2), R("G2", r, 12, 2), 1.0 / 128, ALU.mult, (D2, D3)[r], ALU.min)
+        for r in range(0 if last else 2):
+            ts(R("SA", r, 12, 2), R("G1", r, 12, 2), 1.0 / 128, ALU.mult, (IL, TH)[r], ALU.max)
         while extra:
             idle()
-        for i in range(11, -1, -1):
-            tt(ind(R("TB", T2, TE), col("SB", 2 * i)), R("HH", 16 * i, 16 * i + 16), full("NG", 16), ALU.add)
+        for i in range(5, -1, -1):
+            tt(ind(R("TB", T2, TE), R("SB", 2 * i, 2 * i + 2)), R("HH", 32 * i, 32 * i + 32), full("NG", 32), ALU.add)
             if not last:
-                tt(ind(R("TB", 0, T2), col("SA", 2 * i)), R("HH", 16 * i, 16 * i + 16), full("NG", 16), ALU.add)
-            elif i == 11:
+                tt(ind(R("TB", 0, T2), R("SA", 2 * i, 2 * i + 2)), R("HH", 32 * i, 32 * i + 32), full("NG", 32), ALU.add)
+            elif i == 5:
                 cp(full("CB", L), ind(full("NX", 2 * W), qw))
                 dma("y", T.yc[:], T.CB[0:128:16, :], [full("CB", L)], [], "oyc")
-            elif 5 <= i < 9:
-                turn(192 * (8 - i), 192 * (9 - i))
-            elif i == 4:
+            elif i > 0:
+                turn(192 * (4 - i), 192 * (5 - i))
+            if last and i == 0:
                 act(full("FO", 384), ind(full("TO", 768), full("LF", 24)), ACT.Identity)
-                act(R("PX0", 0, L), full("ZN3", L), ACT.Identity, bias=-12.0)
-                act(R("PX1", 0, L), full("ZN3", L), ACT.Identity, bias=12.0)
                 act(R("PZ", 0, L), R("FO", 0, L), ACT.Identity)
-            elif i == 0:
-                tt(R("PD", 0, L), R("FO", L, 2 * L), R("FO", 0, L), ALU.subtract)
 
     dma("y", T.yx[:], T.TB[:, T2:T2 + W], [R("TB", T2, T2 + W)], [], "oyx")
     arrive("mz", NV - 1)
@@ -603,6 +616,7 @@ def rank_program(g, core, T, topo):
     tt(full("CM", L), full("ZP3", L), R("PX1", 0, L), ALU.is_le)
     mm(R("PT", 0, L), full("GO", 128), full("AD", L), True, False)
     mm(R("PT", 0, L), full("GO", 128), full("CM", L), False, True)
+    tt(R("PD", 0, L), R("FO", L, 2 * L), R("FO", 0, L), ALU.subtract)
     ts(full("FM", L), R("PT", 0, L), 16.0 + 9, ALU.is_ge)
     tt(full("FN", L), full("FM", L), R("PD", 0, L), ALU.mult)
     tt(full("FH", L), full("FN", L), R("PZ", 0, L), ALU.add)

from concourse.mybir import AluOpType, AxisListType, ActivationFunctionType

ALU = AluOpType
ACT = ActivationFunctionType
W, L, NV = 3072, 192, 4
F32, BF, I32, U16 = "float32", "bfloat16", "int32", "uint16"
C0, C2, U0, UH, UF, UN, UP, RBW = 0, 12, 24, 120, 216, 312, 328, 424
T1, T2, TE = 32, 32 + W, 64 + 2 * W


def sb(w, dt=F32):
    return ("sbuf", [128, w], dt)


SCRATCH = {
    "TB": sb(TE, BF), "NX": sb(2 * W, I32), "QW": sb(16, U16), "IW": sb(2 * W), "QF": sb(16), "Q7": sb(16), "RT": sb(384), "JX": sb(384), "QD": sb(24, U16), "XB": sb(32 * L, BF), "EB": sb(32 * L, BF),
    "HC": sb(384, I32), "UC": sb(384), "TI": sb(768), "TO": sb(768),
    "WI": sb(304, I32), "WJ": sb(304, I32), "WF": sb(304), "WG": sb(304), "MM": sb(304), "FO": sb(384),
    "FM": sb(L), "FN": sb(L), "FH": sb(L), "CB": sb(L),
    "OF": sb(384), "OT": sb(384), "OM": sb(384), "OU": sb(384, U16), "PC": sb(4, I32), "PF": sb(16),
    "J16": sb(L), "J12": sb(96), "JG": sb(128), "JA": sb(16), "JB": sb(24), "JC": sb(48), "JD": sb(24),
    "LQ": sb(16, I32), "L1": sb(16), "L2": sb(16), "L3": sb(16), "L4": sb(16), "L5": sb(16),
    "LD": sb(24, U16), "LS0": sb(16, U16), "LK": sb(16, U16), "LR": sb(24, U16), "LE": sb(48, U16), "LF": sb(24, U16),
    "WP": sb(144, BF), "WN": sb(144, BF), "ID": sb(128, BF), "NI": sb(128, BF), "IDF": sb(128),
    "GO": sb(128, BF), "ONB": sb(128, BF), "ONF": sb(128),
    "DG": sb(L), "R0": sb(L), "R2": sb(384), "TIE": sb(384), "KR": sb(96), "RZ": sb(96), "RM": sb(96, BF),
    "MT": sb(128, BF), "ZS": sb(128), "NG": sb(32, BF), "AD": sb(L, BF), "CM": sb(L, BF), "DU": sb(96), "DM": sb(96),
    "KI": sb(16, I32), "KA": sb(16, I32), "KU": sb(16, U16), "SE": sb(L), "SC": sb(L), "CN": sb(L), "S3": sb(L),
    "Q1": sb(16), "QM": sb(16), "QU": sb(16, U16), "QC": sb(16), "Q6": sb(16), "QR": sb(384),
    "DQ": sb(L, BF), "EQ": sb(384), "S2": sb(384), "G1": sb(16), "G2": sb(16),
    "SA": sb(24, U16), "SB": sb(24, U16), "HH": sb(L, BF), "RV": sb(16, I32), "RVB": sb(16, BF),
    "BT": sb(128, BF), "BS": sb(4), "BP": sb(128), "PZ": ("psum", [128, 1024], F32),
}
PSUM = ("PK", "PZ", "PD", "PT", "PM", "PX0", "PX1")
for _b in PSUM:
    SCRATCH.setdefault(_b, ("psum", [128, 512], F32))
for _t in range(NV):
    SCRATCH.update({"RB%d" % _t: sb(RBW), "ZR%d" % _t: sb(4 * L, BF), "ZP%d" % _t: sb(L, BF), "ZN%d" % _t: sb(L, BF), "MS%d" % _t: sb(36)})
TAGS = ("ea", "eb", "ep", "mc", "mz", "mp")
SEMAPHORES = ["qv", "qs", "qt", "qg", "sent", "dmem", "dplc", "dz", "dtb", "dnx", "dtc", "dny", "oyx", "oyz", "oyc", "oyh"] + [
    "%s%d" % (k, t) for t in range(NV) for k in TAGS]


def R(name, lo, hi, step=1, p=None):
    return (name, lo, hi, step, p)


def messages(T, p, t):
    n = len(T.cores)
    nxt, mate = (p + 1) % n, p ^ 3
    rb, rows, zn = "RB%d" % t, R("RB%d" % t, UH - 12, UF - 12), R("ZN%d" % t, 0, L)
    if t == NV - 1:
        return {"eb": (rows, R(rb, UF, UN), mate, 0), "mz": (zn, R("ZP%d" % t, 0, L), mate, 0)}
    nb = "RB%d" % (t + 1)
    m = {"ea": (R(rb, U0, UH - 12), R(nb, U0 + 12, UH), nxt, 1), "eb": (rows, R(nb, UH, UF), nxt, 0),
         "mz": (zn, R("ZR%d" % (t + 1), 0, L), nxt, 0), "mc": (R("MS%d" % t, 0, 36), R(nb, 0, 36), nxt, 1)}
    user = (mate + 1) % n
    if user != p:
        m["ep"] = (rows, R(nb, UP, RBW), user, 0)
        m["mp"] = (zn, R("ZP%d" % t, 0, L), user, 0)
    return m


def first_hop(T, topo, src, dst, h):
    if topo.may_write(src, dst):
        return dst
    able = [c for c in topo.cores_of(src) if c != src and T.rank_of(c) is None and topo.may_write(c, dst)]
    able.sort(key=lambda c: (topo.die(c) != topo.die(src), c))
    return able[h % len(able)]


def helper_program(g, core, T, topo):
    sent = 0
    for t in range(NV):
        for tag in TAGS:
            for p, src in enumerate(T.cores):
                m = messages(T, p, t).get(tag)
                if m is None or first_hop(T, topo, src, T.cores[m[2]], m[3]) != core:
                    continue
                dst = T.cores[m[2]]
                sem = T.sem["%s%d" % (tag, t)]
                piece = T[m[1][0]][:, m[1][1]:m[1][2]]
                g.wait_ge(sem, len(topo.engines(src, core)))
                rid, pid = topo.addr(dst, core)
                g.remote_dma(piece, piece, sem, T.sem.sent, pid, rid, topo.mask(core, dst))
                sent += len(topo.engines(core, dst))
    if sent:
        g.wait_ge(T.sem.sent, sent)


def emit(g, T, ops):
    eng = {"v": g.vector, "s": g.scalar, "t": g.tensor, "g": g, "y": g.sync}
    hist, deps, need = {}, [], set()
    for i, (q, fn, rd, wr, sem) in enumerate(ops):
        d = set()
        for piece, writes in [(r, False) for r in rd] + [(r, True) for r in wr]:
            whole = piece[0] in PSUM
            for j, lo, hi, w, st in hist.get(piece[0], []):
                if not whole and (hi <= piece[1] or piece[2] <= lo or (st == piece[3] and (lo - piece[1]) % st)):
                    continue
                same = ops[j][0] == q and ops[j][4] is None and sem is None
                if not (same and q == "t") and (writes or w or (whole and not same)):
                    d.add(j)
        for piece, writes in [(r, False) for r in rd] + [(r, True) for r in wr]:
            h = hist.setdefault(piece[0], [])
            if writes:
                h[:] = [e for e in h if not (piece[3] == 1 and piece[4] is None and piece[1] <= e[1] and e[2] <= piece[2] and e[0] in d)]
            h.append((i, piece[1], piece[2], writes, piece[3]))
        last = {}
        for j in d:
            if ops[j][4] is None:
                last[ops[j][0]] = max(last.get(ops[j][0], -1), j)
            else:
                last[j] = j
        deps.append(sorted(last.values()))
    seen = {q: {} for q in eng}
    kept = []
    for i, (q, fn, rd, wr, sem) in enumerate(ops):
        k = []
        for j in deps[i]:
            key = ops[j][0] if ops[j][4] is None else ops[j][4][0]
            if q != "x" and seen[q].get(key, -1) < j:
                seen[q][key] = j
                k.append(j)
                need.add(j)
        kept.append(k)
    count, mark, total = {}, {}, {}
    for i, (q, fn, rd, wr, sem) in enumerate(ops):
        if sem is not None:
            total[sem[0]] = sem[1]
            mark[i] = sem
        elif i in need:
            count[q] = count.get(q, 0) + 1
            mark[i] = ("q" + q, count[q])
            total["q" + q] = count[q]
    for i, (q, fn, rd, wr, sem) in enumerate(ops):
        if q == "x":
            continue
        for j in kept[i]:
            eng[q].wait_ge(T.sem[mark[j][0]], mark[j][1])
        ins = fn()
        if sem is None and i in need:
            ins.then_inc(T.sem["q" + q], 1)
    for name in sorted(total):
        g.wait_ge(T.sem[name], total[name])


def rank_program(g, core, T, topo):
    rank = T.rank_of(core)
    if rank is None:
        helper_program(g, core, T, topo)
        return
    n = len(T.cores)
    ops = []
    sent = [0]
    V, S, PE = g.vector, g.scalar, g.tensor

    def ap(r):
        if r[0] == "ind":
            return ap(r[1]).indirect(ap(r[2]))
        ps = slice(None) if r[4] is None else slice(*r[4])
        return T[r[0]][ps, r[1]:r[2]] if r[3] == 1 else T[r[0]][ps, r[1]:r[2]:r[3]]

    def parts(*rs):
        out = []
        for r in rs:
            if isinstance(r, tuple):
                out += [r[1], r[2]] if r[0] == "ind" else [r]
        return out

    def val(x):
        return ap(x) if isinstance(x, tuple) else x

    def rec(q, fn, out, *ins):
        if out[0] == "ind":
            ops.append((q, fn, parts(out[2], *ins), [out[1]], None))
        else:
            ops.append((q, fn, parts(*ins), [out], None))

    def ind(win, off):
        return ("ind", win, off)

    def cp(out, a):
        rec("v", lambda: V.tensor_copy(ap(out), ap(a)), out, a)

    def tt(out, a, b, op):
        rec("v", lambda: V.tensor_tensor(ap(out), ap(a), ap(b), op), out, a, b)

    def ts(out, a, s1, op0, s2=None, op1=None):
        if op1 is None:
            rec("v", lambda: V.tensor_scalar(ap(out), ap(a), val(s1), None, op0), out, a, s1)
        else:
            rec("v", lambda: V.tensor_scalar(ap(out), ap(a), val(s1), val(s2), op0, op1), out, a, s1, s2)

    def fill(out, c):
        rec("v", lambda: V.memset(ap(out), c), out)

    def scan(out, d0, d1):
        rec("v", lambda: V.tensor_tensor_scan(ap(out), ap(d0), ap(d1), 0.0, ALU.mult, ALU.add), out, d0, d1)

    def turn(a, b):
        rec("v", lambda: V.transpose(T.TO[:, a:b], T.TI[:, a:b]), R("TO", a, b), R("TI", a, b))

    def act(out, a, func, bias=0.0, scale=1.0):
        rec("s", lambda: S.activation(ap(out), ap(a), func, bias=val(bias), scale=scale), out, a, bias)

    def mm(out, lhs, rhs, start, stop):
        rec("t", lambda: PE.matmul(ap(out), ap(lhs), ap(rhs), start, stop), out, lhs, rhs)

    def iota(out, pattern, base=0, cm=0):
        if SCRATCH[out[0]][2] == I32:
            rec("g", lambda: g.iota(ap(out), pattern, base, cm), out)
        else:
            rec("g", lambda: g.iota(ap(out), pattern, base, cm, allow_small_or_imprecise_dtypes=True), out)

    def gcopy(out, a):
        rec("g", lambda: g.affine_select(ap(out), ap(a), [[0, a[2] - a[1]]], ALU.is_ge, 0.0, 0, 0), out, a)

    def dma(q, out, a, rd, wr, sem, cnt=16):
        e = g.sync if q == "y" else g.scalar
        ops.append((q, lambda: e.dma_start(out, a).then_inc(T.sem[sem], 16), rd, wr, (sem, cnt)))

    def send(tag, t):
        m = messages(T, rank, t).get(tag)
        if m is None:
            return
        dst = first_hop(T, topo, core, T.cores[m[2]], m[3])
        rid, pid = topo.addr(dst, core)
        sent[0] += len(topo.engines(core, dst))
        ops.append(("g", lambda: g.remote_dma(ap(m[1]), ap(m[0]), T.sem["%s%d" % (tag, t)], T.sem.sent, pid, rid, topo.mask(core, dst)),
                    [m[0]], [], ("sent", sent[0])))

    def arrive(tag, t):
        for p in range(n):
            m = messages(T, p, t).get(tag)
            if m is not None and m[2] == rank:
                hop = first_hop(T, topo, T.cores[p], core, m[3])
                ops.append(("x", None, [], [m[1]], ("%s%d" % (tag, t), len(topo.engines(T.cores[p] if hop == core else hop, core)))))

    def col(name, j, p=None):
        return R(name, j, j + 1, 1, p)

    def full(name, w, p=None):
        return R(name, 0, w, 1, p)

    P12, P13, P1 = (0, 12), (0, 13), (0, 1)
    PP, IL, P31, GB, G0, GB15, D2, TH, BO, BP, I12, TMP, D3 = [col("PF", j) for j in range(13)]

    fill(R("HC", L, 2 * L), 0)
    dma("y", T.HC[:, 0:L], T.mem[:], [], [R("HC", 0, L)], "dmem")
    dma("s", T.ZR0[:, 0:L], T.zt[:], [], [R("ZR0", 0, L)], "dz")
    dma("y", T.HC[0:128:16, L:2 * L], T.plc[:], [], [R("HC", L, 2 * L)], "dplc")
    dma("y", T.TB[:, T1:T2], T.xt[:], [], [R("TB", T1, T2)], "dtb")
    for i in range(16):
        dma("y", T.NX[i:128:16, 0:W], T.nxt[:], [], [R("NX", 0, W)] if i == 15 else [], "dnx", 256)
    dma("y", T.TB[:, T2:T2 + W], T.xt[:], [], [R("TB", T2, T2 + W)], "dtc")

    iota(col("PC", 0), [[0, 1]], 0, 1)
    iota(full("JA", 14), [[16, 14]])
    iota(full("JB", 24), [[16, 12], [0, 2]])
    iota(R("IW", 0, 144), [[1, 144]])
    iota(full("J12", 96, (0, 16)), [[0, 8], [1, 12]])
    iota(full("J16", L), [[0, 12], [1, 16]])
    iota(R("TIE", 0, 192, 1, P1), [[608, 2], [4108, 8], [1, 12]])
    iota(R("TIE", 192, 384, 1, P1), [[608, 2], [4108, 8], [1, 12]], 8 * 4096 + 192)
    fill(full("ONF", 128, P1), 1.0)
    ts(col("PC", 1), col("PC", 0), 15, ALU.bitwise_and)
    ts(col("PC", 2), col("PC", 0), 31, ALU.bitwise_and)
    fill(full("NG", 32), -192.0)
    cp(full("PF", 3), full("PC", 3))
    fill(full("KR", 96, P1), 1024.0)
    ts(full("L1", 14), full("JA", 14), IL, ALU.add)
    ts(full("LD", 24), full("JB", 24), IL, ALU.add)
    ts(GB, PP, IL, ALU.subtract)
    ts(full("LQ", 14), full("L1", 14), -5.5, ALU.add, 1.0 / 12, ALU.mult)
    ts(G0, P31, IL, ALU.subtract)
    ts(GB15, GB, 15.0, ALU.add)
    ts(full("L2", 14), full("LQ", 14), -12.0, ALU.mult)
    ts(full("L3", 14), full("LQ", 14), 2.0, ALU.is_lt, 386.0, ALU.mult)
    ts(D2, IL, float(W), ALU.add)
    tt(full("L2", 14), full("L2", 14), full("L1", 14), ALU.add)
    tt(full("L3", 14), full("L3", 14), full("LQ", 14), ALU.max)
    ts(I12, PP, 12.0, ALU.is_equal)
    ts(full("L4", 14), full("L2", 14), 32.0, ALU.mult, G0, ALU.add)
    cp(R("LK", 0, 6), full("L2", 6))
    ts(R("LK", 6, 12), full("L2", 6), 12.0, ALU.add)
    ts(full("WI", L), R("HC", 0, L), 1, ALU.bitwise_and)
    cp(R("UC", L, 2 * L), R("HC", L, 2 * L))
    tt(full("L5", 14), full("L4", 14), full("L3", 14), ALU.add)
    act(R("TI", 384, 768), ind(R("UC", L, 2 * L), R("LD", 0, 24)), ACT.Identity)
    ts(full("WF", L), full("WI", L), -(2 * W + 1.5), ALU.mult)
    ts(full("ID", 128), R("IW", 0, 128), PP, ALU.is_equal)
    ts(full("LS0", 14), full("L5", 14), -2.0, ALU.add)
    tt(full("WG", L), full("WF", L), R("HC", 0, L), ALU.add)
    act(R("TI", 0, 384), ind(full("WG", L), R("LD", 0, 24)), ACT.Abs, scale=0.5)
    ts(full("WP", 144), R("IW", 0, 144), GB15, ALU.is_equal, 2048.0, ALU.mult)
    ts(full("WN", 144), R("IW", 0, 144), GB15, ALU.is_equal, -1024.0, ALU.mult)
    turn(384, 768)
    ts(full("RZ", 96, P12), full("J12", 96, P12), col("PF", 0, P12), ALU.is_equal, 0.5, ALU.mult)
    ts(full("DG", L), full("J16", L), IL, ALU.is_equal)
    turn(0, 384)
    ts(TH, IL, 16.0, ALU.add)
    ts(D3, IL, W + 16.0, ALU.add)
    cp(R("RB0", 0, 224), ind(full("TO", 768), full("LS0", 14)))

    def later_iotas():
        iota(full("JC", 48), [[0, 2], [1, 12], [0, 2]])
        iota(full("JX", 384), [[0, 6], [-16, 2], [1, 32]])
        iota(full("JD", 24), [[32, 24]])
        iota(full("JG", 128), [[16, 8], [0, 16]])
        for a in range(144, W, 976):
            iota(R("IW", a, a + 976), [[1, 976]], a)

    def spare(t):
        if t == 0:
            return [lambda: ts(full("R0", L), full("J16", L), 1.0, ALU.min),
                    lambda: fill(full("ONB", 128), 1.0),
                    lambda: ts(full("RT", 384), full("JX", 384), IL, ALU.is_equal, 2.0 ** 20 - 1, ALU.mult),
                    lambda: ts(full("NI", 128), R("IW", 0, 128), PP, ALU.is_equal, -1.0, ALU.mult),
                    lambda: act(full("R2", 384), full("RT", 384), ACT.Identity, bias=1.0),
                    lambda: cp(full("LR", 24), full("JC", 24)),
                    lambda: fill(R("R2", 0, 384, 32), 0.0),
                    lambda: ts(full("FM", 96, P13), full("J12", 96, P13), col("PF", 0, P13), ALU.is_equal, col("PF", 10, P13), ALU.max),
                    lambda: ts(full("IDF", 128), R("IW", 0, 128), PP, ALU.is_equal),
                    lambda: fill(full("MT", 128, (0, 16)), 1.0),
                    lambda: ts(full("RM", 96, P13), full("FM", 96, P13), 0.5, ALU.mult)]
        if t == 1:
            return [lambda: ts(TMP, IL, 0.0, ALU.is_equal, 300.0, ALU.mult),
                    lambda: ts(BO, IL, 12.0, ALU.mult, -12.0, ALU.add),
                    lambda: ts(BP, IL, 8.0, ALU.is_ge, 108.0, ALU.mult),
                    lambda: ts(full("GO", 128), full("JG", 128), GB, ALU.is_equal),
                    lambda: ts(BO, BO, TMP, ALU.add),
                    lambda: ts(full("LF", 24), full("JD", 24), P31, ALU.add),
                    lambda: ts(R("LE", 0, 24), R("JC", 0, 24), BO, ALU.add),
                    lambda: ts(R("LE", 24, 48), R("JC", 24, 48), BO, ALU.add, BP, ALU.add)]
        if t == NV - 1:
            u = R("RB3", U0, UN)
            return [lambda: ts(full("WI", 288), u, 4.0, ALU.mult),
                    lambda: ts(full("WJ", 288), full("WI", 288), 1, ALU.bitwise_and),
                    lambda: ts(full("WF", 288), full("WJ", 288), -(W + 0.75), ALU.mult)]
        return []

    def open_keys(t):
        mm(R("PK", 0, 384), full("ONF", 128, P1), full("TIE", 384, P1), True, False)
        if t > 0:
            for a in (96, 288):
                mm(R("PK", a, a + 96), full("BP", 128, P1), full("KR", 96, P1), False, False)

    open_keys(0)
    for t in range(NV):
        rb, zr, zn, ms = "RB%d" % t, "ZR%d" % t, "ZN%d" % t, "MS%d" % t
        z = R(zr, 0, L)
        last = t == NV - 1
        win = R("TB", T1, T2 if t == 0 else T2 + W)
        own_partner = t > 0 and (((rank - 1) % n) ^ 3) == rank
        zp = R("ZN%d" % (t - 1), 0, L) if own_partner else R("ZP%d" % max(t - 1, 0), 0, L)

        def offsets(h, kind):
            a = 192 * h + 96 * kind
            tt(R("OF", a, a + 96), ind(R(rb, 0, U0 if kind else C2), R("LK", 6 * kind, 6 * kind + 6)), R(rb, U0 + 96 * h, UH + 96 * h),
               ALU.subtract if kind else ALU.add)

        def lists(*pieces):
            if t == 0:
                for a, b in pieces:
                    ts(R("OT", a, b), R("OF", a, b), float(W), ALU.is_ge, float(W), ALU.mult)
                for a, b in pieces:
                    tt(R("OM", a, b), R("OF", a, b), R("OT", a, b), ALU.subtract)
            for a, b in pieces:
                cp(R("OU", a, b), R("OM" if t == 0 else "OF", a, b))

        def g_a(a, b):
            tt(R("XB", L * a, L * b), ind(win, R("OU", 12 * a, 12 * b)), R(zr, 0, L * (b - a)), ALU.subtract)

        def abs_a(a, b):
            act(R("EB", L * a, L * b), R("XB", L * a, L * b), ACT.Abs, scale=0.5)

        def g_b(a, b):
            act(R("XB", L * a, L * b), ind(win, R("OU", 12 * a, 12 * b)), ACT.Identity)

        def max_b(a, b):
            tt(R("EB", L * a, L * b), R("XB", L * a, L * b), R("PZ", 0, L * (b - a)), ALU.max)

        def sums(buf, a, b, stop=False):
            for i in range(16):
                mm(R("PK", 12 * a, 12 * b), R("WP" if buf == "EB" else "WN", 15 - i, 143 - i), R(buf, L * a + i, L * b, 16),
                   False, stop and i == 15)

        def turned(src, base):
            for i in range(16):
                mm(R("PT", base + i, base + 128, 16, P12), R(src[0], i, L, 16), R("WP", 15, 143, 16), True, True)

        if t > 0:
            for tag in ("mc", "mz", "mp"):
                arrive(tag, t - 1)
            if t == 1:
                dma("y", T.NX[:, W:2 * W], T.NX[:, 0:W], [R("NX", 0, W), R(rb, C0, C2), z], [R("NX", W, 2 * W)], "dny")
            offsets(0, 0)
            offsets(0, 1)
            lists((0, 96), (96, 192))
        else:
            offsets(0, 0)
            ts(R(rb, C2, U0), R(rb, C0, C2), W + 0.25, ALU.add)
            ts(R("OT", 0, 96), R("OF", 0, 96), float(W), ALU.is_ge, float(W), ALU.mult)
            offsets(0, 1)
            tt(R("OM", 0, 96), R("OF", 0, 96), R("OT", 0, 96), ALU.subtract)
            ts(R("OT", 96, 192), R("OF", 96, 192), float(W), ALU.is_ge, float(W), ALU.mult)
            cp(R("OU", 0, 96), R("OM", 0, 96))
            tt(R("OM", 96, 192), R("OF", 96, 192), R("OT", 96, 192), ALU.subtract)
            cp(R("OU", 96, 192), R("OM", 96, 192))
        gcopy(R(zr, L, 2 * L), z)
        gcopy(R(zr, 2 * L, 4 * L), R(zr, 0, 2 * L))
        if t > 0:
            mm(R("PD", 0, L), full("ID", 128), z, True, False)
            mm(R("PD", 0, L), full("NI", 128), zp, False, True)
        for a, b in ((0, 192), (192, 384), (384, 512), (512, 576), (576, 768)):
            mm(R("PZ", a, b), full("ID", 128), R(zr, a % L, a % L + b - a), True, True)
        turned(z, 128)
        g_b(0, 4)
        if t > 0:
            cp(R("XB", L * 4, L * 8), ind(win, R("OU", 48, 96)))
            act(full("AD", L), R("PD", 0, L), ACT.Abs)
            act(full("ZS", 128, P12), R("PT", 128, 256, 1, P12), ACT.Identity)
            act(full("CM", L), full("AD", L), ACT.Sign, bias=12.5, scale=-1.0)
            for j in range(2):
                mm(R("PX%d" % j, 0, 384), full("ID", 128), R("XB", L * (4 + 2 * j), L * (6 + 2 * j)), True, False)
                for i in range(2):
                    mm(R("PX%d" % j, L * i, L * i + L), full("NI", 128), z, False, i == 1)
                if j == 0:
                    turned(full("CM", L), 0)
            act(R("EB", L * 4, L * 6), R("PX0", 0, 384), ACT.Abs, scale=0.5)
            act(full("MT", 128, P12), R("PT", 0, 128, 1, P12), ACT.Sign, bias=-2048.0)
            mm(R("PM", 0, 96), full("MT", 128, P13), full("RM", 96, P13), True, True)
            act(R("EB", L * 6, L * 8), R("PX1", 0, 384), ACT.Abs, scale=0.5)
            send("ea", t)
        else:
            g_a(4, 8)
            act(full("ZS", 128, P12), R("PT", 128, 256, 1, P12), ACT.Identity)
            abs_a(4, 8)
            send("ea", t)
            send("eb", t)
            send("ep", t)
            later_iotas()
        for a in (48, 288):
            mm(R("PK", a, a + 96), full("ZS", 128, P12), full("RZ", 96, P12), False, False)
        max_b(0, 4)
        sums("XB", 0, 4)
        g_b(12, 16)
        if t > 0:
            g_a(10, 12)
            g_a(9, 10)
            tt(full("DM", 96), full("DU", 96), R("PM", 0, 96), ALU.mult)
            g_a(8, 9)
            tt(R(rb, UH, UF), R(rb, UH, UF), full("DM", 96), ALU.add)
            send("eb", t)
            send("ep", t)
        else:
            g_a(8, 12)
        offsets(1, 0)
        offsets(1, 1)
        lists((192, 288), (288, 384))
        sums("XB", 12, 16)
        abs_a(8, 12)
        max_b(12, 16)
        g_b(16, 20)
        sums("EB", 0, 16)
        g_a(28, 32)
        sums("XB", 16, 20)
        g_b(20, 24)
        max_b(16, 20)
        sums("EB", 16, 20)
        sums("XB", 20, 24)
        abs_a(28, 32)
        g_a(24, 28)
        sums("EB", 28, 32)
        abs_a(24, 28)
        max_b(20, 24)
        sums("EB", 20, 28, True)
        if last:
            arrive("eb", t)
        extra = spare(t)
        early = (5, 3, 0, 0)[t]
        for f in extra[:early]:
            f()
        extra = extra[early:]

        def idle():
            if extra:
                extra.pop(0)()

        if t == 1:
            act(R("IW", W + 2048, 2 * W), R("IW", 2048, W), ACT.Identity)

        for i in range(12):
            rec("v", lambda i=i: V.tensor_reduce(T.KI[:, i:i + 1], T.PK[:, i:384:12], AxisListType.X, ALU.min), col("KI", i), R("PK", 0, 384))
        idle()
        ts(full("KA", 12), full("KI", 12), 511, ALU.bitwise_and)
        if not last:
            ts(full("RV", 12), full("KI", 12), 512, ALU.bitwise_and)
        else:
            idle()
        cp(full("KU", 12), full("KA", 12))
        if not last:
            ts(full("RVB", 12), full("RV", 12), 1.0, ALU.is_ge)
            for i in range(12):
                mm(R("PT", 0, 128, 1, P1), col("RVB", i), full("ONB", 128), i == 0, i == 11)
            act(full("BT", 128, P1), R("PT", 0, 128, 1, P1), ACT.Identity, bias=192.0 - 31.0 / 64, scale=1.0 / 32)
            act(col("BS", 0, P1), R("PT", 0, 1, 1, P1), ACT.Identity, bias=32.0 * 192)
            act(full("BP", 128, P1), full("BT", 128, P1), ACT.Identity, bias=col("BS", 0, P1), scale=-32.0)
            open_keys(t + 1)
        tt(full("SE", L), ind(full("OF", 384), full("KU", 12)), full("DG", L), ALU.mult)
        idle()
        scan(full("SC", L), full("R0", L), full("SE", L))
        if last:
            mm(R("PM", 0, 288), full("IDF", 128), R(rb, U0, UN), True, False)
            mm(R("PM", 0, 288), full("IDF", 128), full("WF", 288), False, True)
            act(full("MM", 288), R("PM", 0, 288), ACT.Abs, scale=2.0)
        qv = R("SC", 15, L, 16)
        un = R(rb, UN, UN + 12) if last else R(ms, 24, 36)
        if t > 0:
            cp(full("QW", 12), qv)
        ts(full("Q1", 12), qv, float(W), ALU.is_ge, float(W), ALU.mult)
        tt(un, qv, R(rb, C0, C2), ALU.subtract)
        if t == 0:
            tt(full("QM", 12), qv, full("Q1", 12), ALU.subtract)
            idle()
            cp(full("QU", 12), full("QM", 12))
        qw = full("QW" if t > 0 else "QU", 12)

        def pairs(r):
            for i in range(2):
                cp(R("QD", 2 * r + i, 24, 4), R(qw[0], i, 12, 2))

        if not last:
            tt(full("CN", L), ind(full("NX", 2 * W if t > 0 else W), qw), full("DG", L), ALU.mult)
            cp(full("QF" if t > 0 else "QC", 12), qw)
            pairs(0)
            scan(full("S3", L), full("R0", L), full("CN", L))
            if t > 0:
                tt(full("QC", 12), full("QF", 12), full("Q1", 12), ALU.subtract)
            pairs(1)
            cp(R(ms, 0, 12), R("S3", 15, L, 16))
            act(R(ms, 12, 24), R("S3", 15, L, 16), ACT.Identity, bias=W + 0.25)
            send("mc", t)
            act(full("QR", 384), ind(full("QC", 12), full("LR", 24)), ACT.Identity)
        else:
            cp(full("QF", 12), qw)
        tt(full("DQ", L), ind(win, qw), z, ALU.subtract)
        if last:
            tt(full("QC", 12), full("QF", 12), full("Q1", 12), ALU.subtract)
            ts(R("WI", 288, 300), un, 4.0, ALU.mult)
        act(full(zn, L), full("DQ", L), ACT.Abs)
        send("mz", t)
        send("mp", t)
        if last:
            act(full("QR", 384), ind(full("QC", 12), full("LR", 24)), ACT.Identity)
            pairs(0)
            pairs(1)
            ts(R("WJ", 288, 300), R("WI", 288, 300), 1, ALU.bitwise_and)
            ts(full("Q7", 12), full("QC", 12), 128.0, ALU.mult)
            ts(R("WF", 288, 300), R("WJ", 288, 300), -(W + 0.75), ALU.mult)
            dma("y", T.yz[:], T[zn][:], [full(zn, L)], [], "oyz")
        else:
            ts(full("Q7", 12), full("QC", 12), 128.0, ALU.mult)
            ts(full("Q6", 12), full("QC", 12), 128.0, ALU.mult, 128.0 * T1 + 48, ALU.add)
        mm(R("PD", 0, L), full("ID", 128), full("DQ", L), True, False)
        mm(R("PD", 0, L), full("ID", 128), z, False, False)
        mm(R("PD", 0, L), full("ID", 128), z, False, True)
        act(full("HH", L), R("PD", 0, L), ACT.Identity, bias=191.75, scale=0.5)
        if last:
            tt(R("WG", 288, 300), R("WF", 288, 300), un, ALU.add)
            act(R("MM", 288, 300), R("WG", 288, 300), ACT.Abs, scale=2.0)
            act(full("TI", 768), ind(full("MM", 300), full("LE", 48)), ACT.Identity)
            act(R("PX0", 0, L), full("ZN3", L), ACT.Identity, bias=-12.0)
            act(R("PX1", 0, L), full("ZN3", L), ACT.Identity, bias=12.0)
        tt(full("EQ", 384), ind(full("IW", 2 * W if t > 0 else W), full("QD", 24)), full("QR", 384), ALU.is_equal)
        idle()
        scan(full("S2", 384), full("R2", 384), full("EQ", 384))
        idle()
        if not last:
            for tag in ("ea", "eb", "ep"):
                arrive(tag, t)
            mine = ((rank ^ 3) + 1) % n == rank
            act(full("DM", 96), R("RB%d" % (t + 1), UH, UF), ACT.Identity, scale=-1.0)
            mm(R("PM", 0, 96), full("IDF", 128), R(rb, UH - 12, UF - 12) if mine else R("RB%d" % (t + 1), UP, RBW), True, False)
            mm(R("PM", 0, 96), full("IDF", 128), full("DM", 96), False, True)
            act(full("DU", 96), R("PM", 0, 96), ACT.Identity)
            if t == 0:
                act(R("IW", W, W + 2048), R("IW", 0, 2048), ACT.Identity)
        bits = R("S2", 31, 384, 32)
        tt(full("G2", 12), full("Q7", 12), bits, ALU.add)
        if not last:
            tt(full("G1", 12), full("Q6", 12), bits, ALU.subtract)
        for r in range(2):
            ts(R("SB", r, 12, 2), R("G2", r, 12, 2), 1.0 / 128, ALU.mult, (D2, D3)[r], ALU.min)
        for r in range(0 if last else 2):
            ts(R("SA", r, 12, 2), R("G1", r, 12, 2), 1.0 / 128, ALU.mult, (IL, TH)[r], ALU.max)
        while extra:
            idle()
        for i in range(5, -1, -1):
            tt(ind(R("TB", T2, TE), R("SB", 2 * i, 2 * i + 2)), R("HH", 32 * i, 32 * i + 32), full("NG", 32), ALU.add)
            if not last:
                tt(ind(R("TB", 0, T2), R("SA", 2 * i, 2 * i + 2)), R("HH", 32 * i, 32 * i + 32), full("NG", 32), ALU.add)
            elif i == 5:
                cp(full("CB", L), ind(full("NX", 2 * W), qw))
                dma("y", T.yc[:], T.CB[0:128:16, :], [full("CB", L)], [], "oyc")
            elif i > 0:
                turn(192 * (4 - i), 192 * (5 - i))
            if last and i == 0:
                act(full("FO", 384), ind(full("TO", 768), full("LF", 24)), ACT.Identity)
                act(R("PZ", 0, L), R("FO", 0, L), ACT.Identity)

    dma("y", T.yx[:], T.TB[:, T2:T2 + W], [R("TB", T2, T2 + W)], [], "oyx")
    arrive("mz", NV - 1)
    tt(full("AD", L), full("ZP3", L), R("PX0", 0, L), ALU.is_ge)
    tt(full("CM", L), full("ZP3", L), R("PX1", 0, L), ALU.is_le)
    mm(R("PT", 0, L), full("GO", 128), full("AD", L), True, False)
    mm(R("PT", 0, L), full("GO", 128), full("CM", L), False, True)
    tt(R("PD", 0, L), R("FO", L, 2 * L), R("FO", 0, L), ALU.subtract)
    ts(full("FM", L), R("PT", 0, L), 16.0 + 9, ALU.is_ge)
    tt(full("FN", L), full("FM", L), R("PD", 0, L), ALU.mult)
    tt(full("FH", L), full("FN", L), R("PZ", 0, L), ALU.add)
    dma("y", T.yh[:], T.FH[:], [full("FH", L)], [], "oyh")
    emit(g, T, ops)
